import numpy as np
import ml_dtypes


def mxq(x, axis, fmt="e4m3"):
    dtype, down = {"e4m3": (ml_dtypes.float8_e4m3fn, 7), "e5m2": (ml_dtypes.float8_e5m2, 14)}[fmt]
    v = np.moveaxis(np.asarray(x, np.float32).astype(ml_dtypes.bfloat16).astype(np.float64), axis, -1)
    blocks = v.reshape(v.shape[:-1] + (-1, 32))
    amax = np.abs(blocks).max(-1, keepdims=True)
    byte = np.maximum(np.where(amax > 0, np.frexp(amax)[1] - 1 + 127, 0) - down, 1)
    scale = np.exp2(byte - 127.0)
    codes = (blocks / scale).astype(np.float32).astype(dtype).astype(np.float64)
    return np.moveaxis((codes * scale).reshape(v.shape), -1, axis)


WIDE = False


def mx_kscale(k):
    if not WIDE:
        return np.ones(k)
    levels = np.array([10, -10, 5, -5, 0])
    if k % 512:
        return np.exp2(np.random.permutation(np.resize(levels, k // 32))).repeat(32)
    a = np.empty((k // 512, 16))
    for p in range(k // 512):
        a[p, :8] = np.random.permutation(np.resize(levels, 8))
        for g in range(8):
            far = levels[np.abs(levels - a[p, g]) >= 10]
            a[p, g + 8] = far[np.random.randint(len(far))]
    return np.exp2(a.ravel()).repeat(32)


def f64(x):
    return np.asarray(x).astype(np.float64)


def striped(idx):
    return np.tile(idx.reshape(-1, 16).T, (8, 1)).astype(np.uint16)


def unstriped(offs):
    return offs[:16].T.reshape(-1).astype(np.int64)


E2M1 = np.array([0.0, 0.5, 1.0, 1.5, 2.0, 3.0, 4.0, 6.0, -0.0, -0.5, -1.0, -1.5, -2.0, -3.0, -4.0, -6.0])


def pack_weight(w, fmt):
    k, n = w.shape
    w = f64(np.asarray(w, np.float32).astype(ml_dtypes.bfloat16)).reshape(k // 32, 32, n)
    amax = np.abs(w).max(1)
    if fmt == "e4m3":
        byte = np.frexp(amax)[1] - 1 + 127 - 7
    else:
        mant, ex = np.frexp(amax / 6.0)
        byte = np.where(mant > 0.5, ex, ex - 1) + 127
    byte = np.clip(np.where(amax > 0, byte, 1), 1, 254)
    scaled = (w * np.exp2(127.0 - byte)[:, None, :]).reshape(k, n).astype(np.float32)
    by_word = np.ascontiguousarray(scaled.reshape(k // 512, 128, 4, n).transpose(0, 1, 3, 2))
    if fmt == "e4m3":
        words = by_word.astype(ml_dtypes.float8_e4m3fn).view(np.uint8)
    else:
        c = by_word.astype(ml_dtypes.float4_e2m1fn).view(np.uint8) & 0xF
        words = (c[..., 0::2] | (c[..., 1::2] << 4)).reshape(k // 512, 128, 2 * n)
    return np.ascontiguousarray(words), np.ascontiguousarray(byte.astype(np.uint8).reshape(k // 512, 16, n))


def unpack_weight(words, scales, fmt):
    g, _, n = scales.shape
    words = np.ascontiguousarray(words).reshape(g, 128, n, -1)
    if fmt == "e4m3":
        vals = words.view(ml_dtypes.float8_e4m3fn).astype(np.float64)
    else:
        nib = np.empty((g, 128, n, 4), np.uint8)
        nib[..., 0::2] = words & 0xF
        nib[..., 1::2] = words >> 4
        vals = E2M1[nib]
    vals = vals * np.repeat(np.exp2(scales.astype(np.float64) - 127.0), 8, axis=1)[..., None]
    return vals.transpose(0, 1, 3, 2).reshape(g * 512, n)


def relu(v):
    return np.maximum(v, 0.0)


K, T, E, C, H, N = 1024, 640, 10, 128, 512, 256


def by_expert(wq, xq):
    return np.concatenate([wq[e].T @ xq[:, e * C:(e + 1) * C] for e in range(E)], axis=1)


def setup_inputs():
    n = np.random.standard_normal
    s = mx_kscale(K)
    u = mx_kscale(H)
    first = np.random.permutation(np.repeat(np.arange(E), T // E))
    second = (first + 1 + np.random.permutation(np.repeat(np.arange(E - 1), -(-T // (E - 1)))[:T])) % E
    while np.bincount(second, minlength=E).max() != T // E:
        load = np.bincount(second, minlength=E); hi, lo = int(load.argmax()), int(load.argmin())
        t = np.flatnonzero((second == hi) & (first != lo))[0]; second[t] = lo
    slot_token = np.empty(E * C, np.int64); pos = np.empty((2, T), np.int64); fill = np.zeros(E, np.int64)
    place = np.stack([np.random.permutation(C) for _ in range(E)])
    for r, deal in enumerate((first, second)):
        for t in np.random.permutation(T):
            e = deal[t]; j = e * C + place[e, fill[e]]; fill[e] += 1; slot_token[j] = t; pos[r, t] = j
    g = np.random.uniform(0.2, 0.8, T)
    x = pack_weight(n((K, T)) * s[:, None], "e4m3")
    w1 = [pack_weight(m, "e2m1") for m in n((E, K, H)) / np.sqrt(K) / s[None, :, None]]
    w3 = [pack_weight(m, "e2m1") for m in n((E, K, H)) / np.sqrt(K) / s[None, :, None] * u]
    w2 = pack_weight(n((H, N)) / np.sqrt(H) / u[:, None], "e2m1")
    return {
        "x_words": x[0],
        "x_scales": x[1],
        "w1_words": np.stack([m[0] for m in w1]),
        "w1_scales": np.stack([m[1] for m in w1]),
        "w3_words": np.stack([m[0] for m in w3]),
        "w3_scales": np.stack([m[1] for m in w3]),
        "w2_words": w2[0],
        "w2_scales": w2[1],
        "gate": np.stack([np.tile(g, (128, 1)), np.tile(1.0 - g, (128, 1))]).astype(np.float32),
        "offs": striped(slot_token),
        "pos1": striped(pos[0]),
        "pos2": striped(pos[1]),
    }


def reference(x_words, x_scales, w1_words, w1_scales, w3_words, w3_scales, w2_words, w2_scales, gate, offs, pos1, pos2):
    w1 = np.stack([unpack_weight(w1_words[e], w1_scales[e], "e2m1") for e in range(E)])
    w3 = np.stack([unpack_weight(w3_words[e], w3_scales[e], "e2m1") for e in range(E)])
    w2 = unpack_weight(w2_words, w2_scales, "e2m1")
    idx = unstriped(offs)
    xq = unpack_weight(x_words, x_scales, "e4m3")[:, idx]
    h = relu(by_expert(w1, xq)) * by_expert(w3, xq)
    c = sum(f64(gate[r, :1]) * h[:, unstriped(p)] for r, p in enumerate((pos1, pos2)))
    return w2.T @ mxq(c, 0, "e4m3")

@@ -1,0 +1,237 @@
+from contextlib import ExitStack
+
+import concourse.mybir as mybir
+from concourse.masks import make_identity
+
+K, T, E, C, H, N = 1024, 640, 10, 128, 512, 256
+FLOPS = 2 * 2 * K * H * E * C + 2 * H * N * T
+
+F32 = mybir.dt.float32
+BF16 = mybir.dt.bfloat16
+I32 = mybir.dt.int32
+U32 = mybir.dt.uint32
+U16 = mybir.dt.uint16
+U8 = mybir.dt.uint8
+FP8X4 = mybir.dt.float8_e4m3fn_x4
+FP4X4 = mybir.dt.float4_e2m1fn_x4
+MULT = mybir.AluOpType.mult
+RELU = mybir.ActivationFunctionType.Relu
+
+P = 128
+S = E * C
+PASSES = K // 512
+HQ = H // P
+SCALE_PARTS = ((0, 2), (2, 4))
+WORD_PARTS = ((0, 2), (2, 4))
+WORD_EXPERTS = 2
+GROUPS = ((0, 4), (4, 8), (8, 10))
+GATHER = 256
+LAST_CHUNKS = ((0, 256), (256, 512), (512, 640))
+
+
+def tile_moe_sdn_glu_relu_kernel(
+    tc, x_words, x_scales, w1_words, w1_scales, w3_words, w3_scales, w2_words, w2_scales, gate, offs, pos1, pos2, out
+):
+    nc = tc.nc
+    with ExitStack() as ctx:
+        keep = ctx.enter_context(tc.tile_pool(name="keep", bufs=1))
+        ring = ctx.enter_context(tc.tile_pool(name="ring", bufs=2))
+        psum = ctx.enter_context(tc.psum_pool(name="psum", bufs=2))
+
+        offs_t = keep.tile([P, S // 16], U16, name="offs_t")
+        pos_t = [keep.tile([P, T // 16], U16, name=f"pos_t{r}") for r in range(2)]
+        xw = [keep.tile([P, T], I32, name=f"xw{s}", align_bytes=64) for s in range(PASSES)]
+        xs = keep.tile([P, PASSES, T], U8, name="xs", align_bytes=64)
+        w2w = keep.tile([P, 2 * N], U8, name="w2w", align_bytes=64)
+        w2s = keep.tile([P, N], U8, name="w2s", align_bytes=64)
+        gate_t = keep.tile([P, 2, T], F32, name="gate_t")
+        ident = keep.tile([P, P], F32, name="ident")
+        gx = [keep.tile([P, S], U32, name=f"gx{s}", align_bytes=64) for s in range(PASSES)]
+        gs = [keep.tile([P, S], U8, name=f"gs{s}", align_bytes=64) for s in range(PASSES)]
+        h = [keep.tile([P, S], F32, name=f"h{q}") for q in range(HQ)]
+        ct = [keep.tile([P, 2, P, 2], BF16, name=f"ct{j}", align_bytes=64) for j in range(T // P)]
+
+        planes = {}
+        words = {}
+        nc.vector.memset(xs[:].bitcast(I32), 0)
+        for q0, q1 in SCALE_PARTS:
+            for m in range(2):
+                plane = keep.tile([P, E * PASSES, (q1 - q0) * P], U8, name=f"plane{q0}_{m}", align_bytes=64)
+                zeroer = nc.gpsimd if (q0, m) == (0, 1) else nc.vector
+                zeroer.memset(plane[:].bitcast(I32), 0)
+                for q in range(q0, q1):
+                    planes[q, m] = (plane, q - q0)
+        nc.vector.memset(w2s[:].bitcast(I32), 0)
+        make_identity(nc, ident[:])
+
+        def load_words(part, e0, step):
+            q0, q1 = part
+            e1 = e0 + WORD_EXPERTS
+            tiles = [
+                ring.tile(
+                    [P, WORD_EXPERTS * PASSES, (q1 - q0) * 2 * P],
+                    U8,
+                    name=f"w{m}",
+                    tag=f"w{m}",
+                    bufs=E // WORD_EXPERTS,
+                    align_bytes=64,
+                )
+                for m in range(2)
+            ]
+            for e in range(e0, e1, step):
+                for m, src in enumerate((w1_words, w3_words)):
+                    rows = src[e : e + step].rearrange("e s p b -> p (e s) b")[:, :, 2 * P * q0 : 2 * P * q1]
+                    dst = tiles[m][:, (e - e0) * PASSES : (e - e0 + step) * PASSES, :]
+                    nc.sync.dma_start(dst.bitcast(I32), rows.bitcast(I32))
+            for m in range(2):
+                for q in range(q0, q1):
+                    for e in range(e0, e1):
+                        words[q, m, e] = (tiles[m], q - q0, e - e0)
+
+        def load_scales(part):
+            q0, q1 = part
+            for m, src in enumerate((w1_scales, w3_scales)):
+                rows = src.rearrange("e s (b r) i -> r b (e s) i", r=4)
+                for r in range(4):
+                    nc.sync.dma_start(
+                        planes[q0, m][0][r:P:32, :, :].bitcast(I32), rows[r][:, :, P * q0 : P * q1].bitcast(I32)
+                    )
+
+        nc.sync.dma_start(offs_t[:], offs)
+        for s in range(PASSES):
+            src = x_words[s].rearrange("p t d -> p (t d)").bitcast(I32)
+            for c0 in range(0, T, T // 2):
+                nc.sync.dma_start(xw[s][:, c0 : c0 + T // 2], src[:, c0 : c0 + T // 2])
+        xs_rows = x_scales.rearrange("s (b r) t -> r b s t", r=4)
+        for r in range(4):
+            nc.sync.dma_start(xs[r:P:32, :, :].bitcast(I32), xs_rows[r].bitcast(I32))
+        load_scales(SCALE_PARTS[0])
+        for r, pos in enumerate((pos1, pos2)):
+            nc.sync.dma_start(pos_t[r][:], pos)
+        nc.sync.dma_start(w2w[:].bitcast(I32), w2_words[0].bitcast(I32))
+        for e0 in range(0, E, WORD_EXPERTS):
+            load_words(WORD_PARTS[0], e0, 1 if e0 < 4 else WORD_EXPERTS)
+        nc.sync.dma_start(gate_t[:], gate.rearrange("r p t -> p r t"))
+        load_scales(SCALE_PARTS[1])
+        w2_rows = w2_scales[0].rearrange("(b r) n -> r b n", r=4)
+        for r in range(4):
+            nc.sync.dma_start(w2s[r:P:32, :].bitcast(I32), w2_rows[r].bitcast(I32))
+
+        def gather_tokens(j):
+            cols = slice(j * GATHER, (j + 1) * GATHER)
+            lst = offs_t[:, j * GATHER // 16 : (j + 1) * GATHER // 16]
+            for s in range(PASSES):
+                nc.vector.tensor_copy(gx[s][:, cols], xw[s][:].bitcast(U32).indirect(lst))
+            for s in range(PASSES):
+                nc.vector.tensor_copy(gs[s][:, cols], xs[:, s, :].indirect(lst))
+
+        def unit(q, g):
+            e0, e1 = GROUPS[g]
+            banks = []
+            for m in range(2):
+                bank = psum.tile([P, (e1 - e0) * C], F32, name=f"acc{m}", tag=f"acc{m}", bufs=2 + m)
+                plane, pq = planes[q, m]
+                for e in range(e0, e1):
+                    wt, wq, we = words[q, m, e]
+                    slots = slice(e * C, (e + 1) * C)
+                    for s in range(PASSES):
+                        nc.tensor.matmul_mx(
+                            out=bank[:, (e - e0) * C : (e - e0 + 1) * C],
+                            lhsT=wt[:, we * PASSES + s, 2 * P * wq : 2 * P * (wq + 1)].bitcast(FP4X4),
+                            lhsT_scale=plane[:, e * PASSES + s, P * pq : P * (pq + 1)],
+                            rhs=gx[s][:, slots].bitcast(FP8X4),
+                            rhs_scale=gs[s][:, slots],
+                            start=(s == 0),
+                            stop=(s == PASSES - 1),
+                        )
+                banks.append(bank)
+            ra = ring.tile([P, (e1 - e0) * C], F32, name="ra", tag="ra", bufs=4)
+            nc.scalar.activation(ra[:], banks[0][:], RELU)
+            nc.vector.tensor_tensor(h[q][:, e0 * C : e1 * C], banks[1][:], ra[:], MULT)
+
+        def combine(q, t0, t1):
+            n = t1 - t0
+            y = ring.tile([P, 2, n], F32, name="y", tag="y", bufs=4)
+            for r in range(2):
+                nc.vector.tensor_tensor(
+                    y[:, r, :], h[q][:].indirect(pos_t[r][:, t0 // 16 : t1 // 16]), gate_t[:, r, t0:t1], MULT
+                )
+            for j0 in range(0, n // P, 4):
+                tiles = range(j0, min(j0 + 4, n // P))
+                turned = psum.tile([P, len(tiles), P], F32, name="turned", tag="turned", bufs=3)
+                for j in tiles:
+                    for r in range(2):
+                        nc.tensor.matmul(
+                            turned[:, j - j0, :],
+                            lhsT=y[:, r, j * P : (j + 1) * P],
+                            rhs=ident[:],
+                            start=(r == 0),
+                            stop=(r == 1),
+                            is_transpose=True,
+                        )
+                for j in tiles:
+                    nc.scalar.copy(
+                        ct[t0 // P + j][:, :, 32 * q : 32 * (q + 1), :],
+                        turned[:, j - j0, :].rearrange("t (p u e) -> t u p e", u=2, e=2),
+                    )
+
+        out_v = out.rearrange("(a p) t -> p a t", p=P)
+
+        def turn_back(t0, t1):
+            n = t1 - t0
+            grouped = ring.tile([P, n, 4], BF16, name="grouped", tag="grouped", bufs=3, align_bytes=64)
+            for j in range(n // P):
+                pairs = ct[t0 // P + j][:].rearrange("t u p e -> t (u p e)").bitcast(F32)
+                back = psum.tile([P, 2, P], F32, name="back", tag="acc0", bufs=2)
+                for u in range(2):
+                    nc.tensor.transpose(back[:, u, :], pairs[:, u * P : (u + 1) * P], ident[:])
+                nc.scalar.copy(grouped[:, j * P : (j + 1) * P, :].bitcast(F32), back[:].rearrange("p u t -> p t u"))
+            return grouped
+
+        def project(t0, t1, grouped):
+            n = t1 - t0
+            codes = ring.tile([P, n], U32, name="codes", tag="codes", bufs=3, align_bytes=64)
+            cs = ring.tile([P, n], U8, name="cs", tag="cs", bufs=3, align_bytes=64)
+            nc.vector.quantize_mx(
+                out=codes[:].bitcast(FP8X4), scales=cs[:], in_=grouped[:].rearrange("p t j -> p (t j)")
+            )
+            acc = psum.tile([P, 2, n], F32, name="acc_out", tag="acc1", bufs=3)
+            for a in range(2):
+                nc.tensor.matmul_mx(
+                    out=acc[:, a, :],
+                    lhsT=w2w[:, 2 * P * a : 2 * P * (a + 1)].bitcast(FP4X4),
+                    lhsT_scale=w2s[:, P * a : P * (a + 1)],
+                    rhs=codes[:].bitcast(FP8X4),
+                    rhs_scale=cs[:],
+                    start=True,
+                    stop=True,
+                )
+            res = ring.tile([P, 2, n], F32, name="res", tag="res", bufs=3)
+            nc.vector.tensor_copy(res[:], acc[:])
+            nc.sync.dma_start(out_v[:, :, t0:t1], res[:])
+
+        for j in range(4):
+            gather_tokens(j)
+        unit(0, 0)
+        gather_tokens(4)
+        unit(0, 1)
+        unit(1, 0)
+        unit(0, 2)
+        combine(0, 0, T)
+        unit(1, 1)
+        unit(1, 2)
+        combine(1, 0, T)
+        for e0 in range(0, E, WORD_EXPERTS):
+            load_words(WORD_PARTS[1], e0, WORD_EXPERTS)
+        for g in range(2):
+            unit(2, g)
+            unit(3, g)
+        unit(2, 2)
+        combine(2, 0, T)
+        unit(3, 2)
+        made = []
+        for t0, t1 in LAST_CHUNKS:
+            combine(3, t0, t1)
+            made.append((t0, t1, turn_back(t0, t1)))
+        for item in made:
+            project(*item)

@@ -18,14 +18,13 @@ MULT = mybir.AluOpType.mult
 RELU = mybir.ActivationFunctionType.Relu
 
 P = 128
+BANK = 512
 S = E * C
 PASSES = K // 512
 HQ = H // P
-SCALE_PARTS = ((0, 2), (2, 4))
-WORD_PARTS = ((0, 2), (2, 4))
-WORD_EXPERTS = 2
 GROUPS = ((0, 4), (4, 8), (8, 10))
-GATHER = 256
+LOADS = GROUPS
+GATHERS = ((0, 256), (256, 512), (512, 896), (896, 1280))
 LAST_CHUNKS = ((0, 256), (256, 512), (512, 640))
 
 
@@ -35,8 +34,8 @@ def tile_moe_sdn_glu_relu_kernel(
     nc = tc.nc
     with ExitStack() as ctx:
         keep = ctx.enter_context(tc.tile_pool(name="keep", bufs=1))
-        ring = ctx.enter_context(tc.tile_pool(name="ring", bufs=2))
-        psum = ctx.enter_context(tc.psum_pool(name="psum", bufs=2))
+        psum = ctx.enter_context(tc.psum_pool(name="psum", bufs=1))
+        banks = [psum.tile([P, BANK], F32, name=f"bank{b}") for b in range(8)]
 
         offs_t = keep.tile([P, S // 16], U16, name="offs_t")
         pos_t = [keep.tile([P, T // 16], U16, name=f"pos_t{r}") for r in range(2)]
@@ -50,119 +49,105 @@ def tile_moe_sdn_glu_relu_kernel(
         gs = [keep.tile([P, S], U8, name=f"gs{s}", align_bytes=64) for s in range(PASSES)]
         h = [keep.tile([P, S], F32, name=f"h{q}") for q in range(HQ)]
         ct = [keep.tile([P, 2, P, 2], BF16, name=f"ct{j}", align_bytes=64) for j in range(T // P)]
+        planes = [
+            [keep.tile([P, E * PASSES, 2 * P], U8, name=f"plane{half}_{m}", align_bytes=64) for m in range(2)]
+            for half in range(2)
+        ]
+        words = [
+            [keep.tile([P, E * PASSES, 4 * P], U8, name=f"words{half}_{m}", align_bytes=64) for m in range(2)]
+            for half in range(2)
+        ]
 
-        planes = {}
-        words = {}
-        nc.vector.memset(xs[:].bitcast(I32), 0)
-        for q0, q1 in SCALE_PARTS:
-            for m in range(2):
-                plane = keep.tile([P, E * PASSES, (q1 - q0) * P], U8, name=f"plane{q0}_{m}", align_bytes=64)
-                zeroer = nc.gpsimd if (q0, m) == (0, 1) else nc.vector
-                zeroer.memset(plane[:].bitcast(I32), 0)
-                for q in range(q0, q1):
-                    planes[q, m] = (plane, q - q0)
-        nc.vector.memset(w2s[:].bitcast(I32), 0)
+        nc.gpsimd.memset(xs[:].bitcast(I32), 0)
+        nc.vector.memset(planes[0][0][:].bitcast(I32), 0)
+        nc.gpsimd.memset(planes[0][1][:].bitcast(I32), 0)
+        for m in range(2):
+            nc.gpsimd.memset(planes[1][m][:].bitcast(I32), 0)
+        nc.gpsimd.memset(w2s[:].bitcast(I32), 0)
         make_identity(nc, ident[:])
 
-        def load_words(part, e0, step):
-            q0, q1 = part
-            e1 = e0 + WORD_EXPERTS
-            tiles = [
-                ring.tile(
-                    [P, WORD_EXPERTS * PASSES, (q1 - q0) * 2 * P],
-                    U8,
-                    name=f"w{m}",
-                    tag=f"w{m}",
-                    bufs=E // WORD_EXPERTS,
-                    align_bytes=64,
-                )
-                for m in range(2)
-            ]
-            for e in range(e0, e1, step):
-                for m, src in enumerate((w1_words, w3_words)):
-                    rows = src[e : e + step].rearrange("e s p b -> p (e s) b")[:, :, 2 * P * q0 : 2 * P * q1]
-                    dst = tiles[m][:, (e - e0) * PASSES : (e - e0 + step) * PASSES, :]
-                    nc.sync.dma_start(dst.bitcast(I32), rows.bitcast(I32))
-            for m in range(2):
-                for q in range(q0, q1):
-                    for e in range(e0, e1):
-                        words[q, m, e] = (tiles[m], q - q0, e - e0)
+        def load_words(half, e0, e1):
+            for m, src in enumerate((w1_words, w3_words)):
+                rows = src[e0:e1].rearrange("e s p b -> p (e s) b")[:, :, 4 * P * half : 4 * P * (half + 1)]
+                dst = words[half][m][:, e0 * PASSES : e1 * PASSES, :]
+                nc.sync.dma_start(dst.bitcast(I32), rows.bitcast(I32))
 
-        def load_scales(part):
-            q0, q1 = part
+        def load_scales(half, queue):
             for m, src in enumerate((w1_scales, w3_scales)):
                 rows = src.rearrange("e s (b r) i -> r b (e s) i", r=4)
                 for r in range(4):
-                    nc.sync.dma_start(
-                        planes[q0, m][0][r:P:32, :, :].bitcast(I32), rows[r][:, :, P * q0 : P * q1].bitcast(I32)
+                    queue.dma_start(
+                        planes[half][m][r:P:32, :, :].bitcast(I32),
+                        rows[r][:, :, 2 * P * half : 2 * P * (half + 1)].bitcast(I32),
                     )
 
         nc.sync.dma_start(offs_t[:], offs)
-        for s in range(PASSES):
-            src = x_words[s].rearrange("p t d -> p (t d)").bitcast(I32)
-            for c0 in range(0, T, T // 2):
-                nc.sync.dma_start(xw[s][:, c0 : c0 + T // 2], src[:, c0 : c0 + T // 2])
         xs_rows = x_scales.rearrange("s (b r) t -> r b s t", r=4)
         for r in range(4):
             nc.sync.dma_start(xs[r:P:32, :, :].bitcast(I32), xs_rows[r].bitcast(I32))
-        load_scales(SCALE_PARTS[0])
+        for s in range(PASSES):
+            nc.sync.dma_start(xw[s][:], x_words[s].rearrange("p t d -> p (t d)").bitcast(I32))
+        load_scales(0, nc.sync)
+        for e0, e1 in LOADS:
+            load_words(0, e0, e1)
         for r, pos in enumerate((pos1, pos2)):
             nc.sync.dma_start(pos_t[r][:], pos)
-        nc.sync.dma_start(w2w[:].bitcast(I32), w2_words[0].bitcast(I32))
-        for e0 in range(0, E, WORD_EXPERTS):
-            load_words(WORD_PARTS[0], e0, 1 if e0 < 4 else WORD_EXPERTS)
         nc.sync.dma_start(gate_t[:], gate.rearrange("r p t -> p r t"))
-        load_scales(SCALE_PARTS[1])
+        load_scales(1, nc.gpsimd)
+        for e0, e1 in LOADS:
+            load_words(1, e0, e1)
+        nc.sync.dma_start(w2w[:].bitcast(I32), w2_words[0].bitcast(I32))
         w2_rows = w2_scales[0].rearrange("(b r) n -> r b n", r=4)
         for r in range(4):
             nc.sync.dma_start(w2s[r:P:32, :].bitcast(I32), w2_rows[r].bitcast(I32))
 
-        def gather_tokens(j):
-            cols = slice(j * GATHER, (j + 1) * GATHER)
-            lst = offs_t[:, j * GATHER // 16 : (j + 1) * GATHER // 16]
+        def gather_tokens(c0, c1):
+            lst = offs_t[:, c0 // 16 : c1 // 16]
             for s in range(PASSES):
-                nc.vector.tensor_copy(gx[s][:, cols], xw[s][:].bitcast(U32).indirect(lst))
+                nc.vector.tensor_copy(gs[s][:, c0:c1], xs[:, s, :].indirect(lst))
             for s in range(PASSES):
-                nc.vector.tensor_copy(gs[s][:, cols], xs[:, s, :].indirect(lst))
+                nc.vector.tensor_copy(gx[s][:, c0:c1], xw[s][:].bitcast(U32).indirect(lst))
 
-        def unit(q, g):
+        def unit(q, g, pair):
             e0, e1 = GROUPS[g]
-            banks = []
+            width = (e1 - e0) * C
+            sums = keep.tile([P, 2, width], F32, name=f"sums{q}_{g}")
             for m in range(2):
-                bank = psum.tile([P, (e1 - e0) * C], F32, name=f"acc{m}", tag=f"acc{m}", bufs=2 + m)
-                plane, pq = planes[q, m]
+                bank = banks[pair[m]]
+                cols = slice(P * (q % 2), P * (q % 2 + 1))
                 for e in range(e0, e1):
-                    wt, wq, we = words[q, m, e]
                     slots = slice(e * C, (e + 1) * C)
                     for s in range(PASSES):
                         nc.tensor.matmul_mx(
                             out=bank[:, (e - e0) * C : (e - e0 + 1) * C],
-                            lhsT=wt[:, we * PASSES + s, 2 * P * wq : 2 * P * (wq + 1)].bitcast(FP4X4),
-                            lhsT_scale=plane[:, e * PASSES + s, P * pq : P * (pq + 1)],
+                            lhsT=words[q // 2][m][:, e * PASSES + s, 2 * cols.start : 2 * cols.stop].bitcast(FP4X4),
+                            lhsT_scale=planes[q // 2][m][:, e * PASSES + s, cols],
                             rhs=gx[s][:, slots].bitcast(FP8X4),
                             rhs_scale=gs[s][:, slots],
                             start=(s == 0),
                             stop=(s == PASSES - 1),
                         )
-                banks.append(bank)
-            ra = ring.tile([P, (e1 - e0) * C], F32, name="ra", tag="ra", bufs=4)
-            nc.scalar.activation(ra[:], banks[0][:], RELU)
-            nc.vector.tensor_tensor(h[q][:, e0 * C : e1 * C], banks[1][:], ra[:], MULT)
+                if m == 0:
+                    nc.scalar.activation(sums[:, 0, :], bank[:, :width], RELU)
+                else:
+                    nc.scalar.copy(sums[:, 1, :], bank[:, :width])
+            nc.vector.tensor_tensor(h[q][:, e0 * C : e1 * C], sums[:, 0, :], sums[:, 1, :], MULT)
 
-        def combine(q, t0, t1):
-            n = t1 - t0
-            y = ring.tile([P, 2, n], F32, name="y", tag="y", bufs=4)
+        def pick(q, t0, t1):
+            y = keep.tile([P, 2, t1 - t0], F32, name=f"y{q}_{t0}")
             for r in range(2):
                 nc.vector.tensor_tensor(
                     y[:, r, :], h[q][:].indirect(pos_t[r][:, t0 // 16 : t1 // 16]), gate_t[:, r, t0:t1], MULT
                 )
-            for j0 in range(0, n // P, 4):
-                tiles = range(j0, min(j0 + 4, n // P))
-                turned = psum.tile([P, len(tiles), P], F32, name="turned", tag="turned", bufs=3)
+            return y
+
+        def turn(q, t0, t1, y, into):
+            for bank, j0 in zip(into, range(0, (t1 - t0) // P, 4)):
+                tiles = range(j0, min(j0 + 4, (t1 - t0) // P))
                 for j in tiles:
                     for r in range(2):
                         nc.tensor.matmul(
-                            turned[:, j - j0, :],
+                            bank[:, (j - j0) * P : (j - j0 + 1) * P],
                             lhsT=y[:, r, j * P : (j + 1) * P],
                             rhs=ident[:],
                             start=(r == 0),
@@ -172,33 +157,34 @@ def tile_moe_sdn_glu_relu_kernel(
                 for j in tiles:
                     nc.scalar.copy(
                         ct[t0 // P + j][:, :, 32 * q : 32 * (q + 1), :],
-                        turned[:, j - j0, :].rearrange("t (p u e) -> t u p e", u=2, e=2),
+                        bank[:, (j - j0) * P : (j - j0 + 1) * P].rearrange("t (p u e) -> t u p e", u=2, e=2),
                     )
 
         out_v = out.rearrange("(a p) t -> p a t", p=P)
 
-        def turn_back(t0, t1):
+        def turn_back(t0, t1, into):
             n = t1 - t0
-            grouped = ring.tile([P, n, 4], BF16, name="grouped", tag="grouped", bufs=3, align_bytes=64)
+            grouped = keep.tile([P, n, 4], BF16, name=f"grouped{t0}", align_bytes=64)
             for j in range(n // P):
                 pairs = ct[t0 // P + j][:].rearrange("t u p e -> t (u p e)").bitcast(F32)
-                back = psum.tile([P, 2, P], F32, name="back", tag="acc0", bufs=2)
+                back = into[j][:, : 2 * P]
                 for u in range(2):
-                    nc.tensor.transpose(back[:, u, :], pairs[:, u * P : (u + 1) * P], ident[:])
-                nc.scalar.copy(grouped[:, j * P : (j + 1) * P, :].bitcast(F32), back[:].rearrange("p u t -> p t u"))
+                    nc.tensor.transpose(back[:, u * P : (u + 1) * P], pairs[:, u * P : (u + 1) * P], ident[:])
+                nc.scalar.copy(
+                    grouped[:, j * P : (j + 1) * P, :].bitcast(F32), back.rearrange("p (u t) -> p t u", u=2)
+                )
             return grouped
 
-        def project(t0, t1, grouped):
+        def project(t0, t1, grouped, bank):
             n = t1 - t0
-            codes = ring.tile([P, n], U32, name="codes", tag="codes", bufs=3, align_bytes=64)
-            cs = ring.tile([P, n], U8, name="cs", tag="cs", bufs=3, align_bytes=64)
+            codes = keep.tile([P, n], U32, name=f"codes{t0}", align_bytes=64)
+            cs = keep.tile([P, n], U8, name=f"cs{t0}", align_bytes=64)
             nc.vector.quantize_mx(
                 out=codes[:].bitcast(FP8X4), scales=cs[:], in_=grouped[:].rearrange("p t j -> p (t j)")
             )
-            acc = psum.tile([P, 2, n], F32, name="acc_out", tag="acc1", bufs=3)
             for a in range(2):
                 nc.tensor.matmul_mx(
-                    out=acc[:, a, :],
+                    out=bank[:, a * n : (a + 1) * n],
                     lhsT=w2w[:, 2 * P * a : 2 * P * (a + 1)].bitcast(FP4X4),
                     lhsT_scale=w2s[:, P * a : P * (a + 1)],
                     rhs=codes[:].bitcast(FP8X4),
@@ -206,32 +192,34 @@ def tile_moe_sdn_glu_relu_kernel(
                     start=True,
                     stop=True,
                 )
-            res = ring.tile([P, 2, n], F32, name="res", tag="res", bufs=3)
-            nc.vector.tensor_copy(res[:], acc[:])
+            res = keep.tile([P, 2, n], F32, name=f"res{t0}")
+            nc.vector.tensor_copy(res[:], bank[:, : 2 * n].rearrange("p (a t) -> p a t", a=2))
             nc.sync.dma_start(out_v[:, :, t0:t1], res[:])
 
-        for j in range(4):
-            gather_tokens(j)
-        unit(0, 0)
-        gather_tokens(4)
-        unit(0, 1)
-        unit(1, 0)
-        unit(0, 2)
-        combine(0, 0, T)
-        unit(1, 1)
-        unit(1, 2)
-        combine(1, 0, T)
-        for e0 in range(0, E, WORD_EXPERTS):
-            load_words(WORD_PARTS[1], e0, WORD_EXPERTS)
-        for g in range(2):
-            unit(2, g)
-            unit(3, g)
-        unit(2, 2)
-        combine(2, 0, T)
-        unit(3, 2)
+        for c0, c1 in GATHERS:
+            gather_tokens(c0, c1)
+        unit(0, 0, (0, 1))
+        unit(1, 0, (2, 3))
+        unit(0, 1, (4, 5))
+        unit(0, 2, (0, 1))
+        y0 = pick(0, 0, T)
+        unit(1, 1, (0, 3))
+        unit(1, 2, (2, 5))
+        y1 = pick(1, 0, T)
+        unit(2, 0, (4, 1))
+        unit(3, 0, (0, 3))
+        unit(2, 1, (6, 7))
+        unit(2, 2, (4, 1))
+        y2 = pick(2, 0, T)
+        unit(3, 1, (4, 3))
+        unit(3, 2, (0, 7))
+        turn(0, 0, T, y0, (banks[1], banks[4]))
+        turn(1, 0, T, y1, (banks[7], banks[0]))
+        turn(2, 0, T, y2, (banks[3], banks[4]))
+        picked = [pick(HQ - 1, t0, t1) for t0, t1 in LAST_CHUNKS]
         made = []
-        for t0, t1 in LAST_CHUNKS:
-            combine(3, t0, t1)
-            made.append((t0, t1, turn_back(t0, t1)))
-        for item in made:
-            project(*item)
+        for i, (t0, t1) in enumerate(LAST_CHUNKS):
+            turn(HQ - 1, t0, t1, picked[i], [banks[(2, 5, 6)[i]]])
+            made.append(turn_back(t0, t1, [banks[b] for b in ((1, 7), (0, 3), (4,))[i]]))
+        for i, (t0, t1) in enumerate(LAST_CHUNKS):
+            project(t0, t1, made[i], banks[(2, 5, 6)[i]])

@@ -23,6 +23,7 @@ S = E * C
 PASSES = K // 512
 HQ = H // P
 GROUPS = ((0, 4), (4, 8), (8, 10))
+PLANE_EXPERTS = 5
 LOADS = GROUPS
 GATHERS = ((0, 256), (256, 512), (512, 896), (896, 1280))
 LAST_CHUNKS = ((0, 256), (256, 512), (512, 640))
@@ -50,8 +51,8 @@ def tile_moe_sdn_glu_relu_kernel(
         h = [keep.tile([P, S], F32, name=f"h{q}") for q in range(HQ)]
         ct = [keep.tile([P, 2, P, 2], BF16, name=f"ct{j}", align_bytes=64) for j in range(T // P)]
         planes = [
-            [keep.tile([P, E * PASSES, 2 * P], U8, name=f"plane{half}_{m}", align_bytes=64) for m in range(2)]
-            for half in range(2)
+            [keep.tile([P, PLANE_EXPERTS * PASSES, H], U8, name=f"plane{part}_{m}", align_bytes=64) for m in range(2)]
+            for part in range(E // PLANE_EXPERTS)
         ]
         words = [
             [keep.tile([P, E * PASSES, 4 * P], U8, name=f"words{half}_{m}", align_bytes=64) for m in range(2)]
@@ -59,10 +60,9 @@ def tile_moe_sdn_glu_relu_kernel(
         ]
 
         nc.gpsimd.memset(xs[:].bitcast(I32), 0)
-        nc.vector.memset(planes[0][0][:].bitcast(I32), 0)
-        nc.gpsimd.memset(planes[0][1][:].bitcast(I32), 0)
-        for m in range(2):
-            nc.gpsimd.memset(planes[1][m][:].bitcast(I32), 0)
+        for pair in planes:
+            for plane in pair:
+                nc.vector.memset(plane[:].bitcast(I32), 0)
         nc.gpsimd.memset(w2s[:].bitcast(I32), 0)
         make_identity(nc, ident[:])
 
@@ -72,28 +72,23 @@ def tile_moe_sdn_glu_relu_kernel(
                 dst = words[half][m][:, e0 * PASSES : e1 * PASSES, :]
                 nc.sync.dma_start(dst.bitcast(I32), rows.bitcast(I32))
 
-        def load_scales(half, queue):
-            for m, src in enumerate((w1_scales, w3_scales)):
-                rows = src.rearrange("e s (b r) i -> r b (e s) i", r=4)
-                for r in range(4):
-                    queue.dma_start(
-                        planes[half][m][r:P:32, :, :].bitcast(I32),
-                        rows[r][:, :, 2 * P * half : 2 * P * (half + 1)].bitcast(I32),
-                    )
-
         nc.sync.dma_start(offs_t[:], offs)
+        for s in range(PASSES):
+            nc.sync.dma_start(xw[s][:], x_words[s].rearrange("p t d -> p (t d)").bitcast(I32))
         xs_rows = x_scales.rearrange("s (b r) t -> r b s t", r=4)
         for r in range(4):
             nc.sync.dma_start(xs[r:P:32, :, :].bitcast(I32), xs_rows[r].bitcast(I32))
-        for s in range(PASSES):
-            nc.sync.dma_start(xw[s][:], x_words[s].rearrange("p t d -> p (t d)").bitcast(I32))
-        load_scales(0, nc.sync)
+        for part, pair in enumerate(planes):
+            for plane, src in zip(pair, (w1_scales, w3_scales)):
+                some = src[part * PLANE_EXPERTS : (part + 1) * PLANE_EXPERTS]
+                rows = some.rearrange("e s (b r) i -> r b (e s) i", r=4)
+                for r in range(4):
+                    nc.sync.dma_start(plane[r:P:32, :, :].bitcast(I32), rows[r].bitcast(I32))
         for e0, e1 in LOADS:
             load_words(0, e0, e1)
         for r, pos in enumerate((pos1, pos2)):
             nc.sync.dma_start(pos_t[r][:], pos)
         nc.sync.dma_start(gate_t[:], gate.rearrange("r p t -> p r t"))
-        load_scales(1, nc.gpsimd)
         for e0, e1 in LOADS:
             load_words(1, e0, e1)
         nc.sync.dma_start(w2w[:].bitcast(I32), w2_words[0].bitcast(I32))
@@ -121,7 +116,7 @@ def tile_moe_sdn_glu_relu_kernel(
                         nc.tensor.matmul_mx(
                             out=bank[:, (e - e0) * C : (e - e0 + 1) * C],
                             lhsT=words[q // 2][m][:, e * PASSES + s, 2 * cols.start : 2 * cols.stop].bitcast(FP4X4),
-                            lhsT_scale=planes[q // 2][m][:, e * PASSES + s, cols],
+                            lhsT_scale=planes[e // PLANE_EXPERTS][m][:, e % PLANE_EXPERTS * PASSES + s, P * q : P * (q + 1)],
                             rhs=gx[s][:, slots].bitcast(FP8X4),
                             rhs_scale=gs[s][:, slots],
                             start=(s == 0),

@@ -24,7 +24,7 @@ PASSES = K // 512
 HQ = H // P
 GROUPS = ((0, 4), (4, 8), (8, 10))
 PLANE_EXPERTS = 5
-LOADS = GROUPS
+LOADS = ((0, 4), (4, 6), (6, 8), (8, 10))
 GATHERS = ((0, 256), (256, 512), (512, 896), (896, 1280))
 LAST_CHUNKS = ((0, 256), (256, 512), (512, 640))
 
@@ -41,7 +41,7 @@ def tile_moe_sdn_glu_relu_kernel(
         offs_t = keep.tile([P, S // 16], U16, name="offs_t")
         pos_t = [keep.tile([P, T // 16], U16, name=f"pos_t{r}") for r in range(2)]
         xw = [keep.tile([P, T], I32, name=f"xw{s}", align_bytes=64) for s in range(PASSES)]
-        xs = keep.tile([P, PASSES, T], U8, name="xs", align_bytes=64)
+        xs = keep.tile([P, T], U8, name="xs", align_bytes=64)
         w2w = keep.tile([P, 2 * N], U8, name="w2w", align_bytes=64)
         w2s = keep.tile([P, N], U8, name="w2s", align_bytes=64)
         gate_t = keep.tile([P, 2, T], F32, name="gate_t")
@@ -65,6 +65,8 @@ def tile_moe_sdn_glu_relu_kernel(
                 nc.vector.memset(plane[:].bitcast(I32), 0)
         nc.gpsimd.memset(w2s[:].bitcast(I32), 0)
         make_identity(nc, ident[:])
+        gate_rows = keep.tile([P, P], F32, name="gate_rows")
+        nc.gpsimd.memset(gate_rows[:], 0.0)
 
         def load_words(half, e0, e1):
             for m, src in enumerate((w1_words, w3_words)):
@@ -73,22 +75,43 @@ def tile_moe_sdn_glu_relu_kernel(
                 nc.sync.dma_start(dst.bitcast(I32), rows.bitcast(I32))
 
         nc.sync.dma_start(offs_t[:], offs)
+        for b in range(2):
+            nc.sync.dma_start(xs[32 * b : 32 * b + 8, :].bitcast(I32), x_scales[:, 4 * b : 4 * b + 4, :].bitcast(I32))
+        for b in range(2, 4):
+            for s in range(PASSES):
+                first = 32 * b - 4 * s
+                nc.sync.dma_start(xs[first : first + 4, :].bitcast(I32), x_scales[s, 4 * b : 4 * b + 4, :].bitcast(I32))
         for s in range(PASSES):
             nc.sync.dma_start(xw[s][:], x_words[s].rearrange("p t d -> p (t d)").bitcast(I32))
-        xs_rows = x_scales.rearrange("s (b r) t -> r b s t", r=4)
-        for r in range(4):
-            nc.sync.dma_start(xs[r:P:32, :, :].bitcast(I32), xs_rows[r].bitcast(I32))
         for part, pair in enumerate(planes):
             for plane, src in zip(pair, (w1_scales, w3_scales)):
                 some = src[part * PLANE_EXPERTS : (part + 1) * PLANE_EXPERTS]
                 rows = some.rearrange("e s (b r) i -> r b (e s) i", r=4)
                 for r in range(4):
                     nc.sync.dma_start(plane[r:P:32, :, :].bitcast(I32), rows[r].bitcast(I32))
+        for r in range(2):
+            nc.sync.dma_start(gate_rows[4 * r : 4 * r + 4, :], gate[r, 0, :BANK].rearrange("(j t) -> j t", t=P))
+        nc.sync.dma_start(gate_rows[8:10, :], gate[:, 0, BANK:])
+        nc.tensor.transpose(banks[7][:, :P], gate_rows[:], ident[:])
+        gate_cols = keep.tile([P, 16], F32, name="gate_cols")
+        nc.scalar.copy(gate_cols[:], banks[7][:, :16])
+        for b, count in ((4, 4), (5, 4), (6, 2)):
+            for j in range(count):
+                c = 4 * (b - 4) + j
+                nc.tensor.transpose(
+                    banks[b][:, j * P : (j + 1) * P], gate_cols[:, c : c + 1].to_broadcast([P, P]), ident[:]
+                )
+        for r in range(2):
+            nc.scalar.copy(gate_t[:, r, :BANK], banks[4 + r][:])
+        nc.scalar.copy(gate_t[:, :, BANK:], banks[6][:, : 2 * P].rearrange("p (r t) -> p r t", r=2))
+        for c0, c1 in GATHERS:
+            nc.vector.tensor_copy(gs[0][:, c0:c1], xs[:].indirect(offs_t[:, c0 // 16 : c1 // 16]))
+        nc.sync.dma_start(gs[1][0:64, :].bitcast(I32), gs[0][4:68, :].bitcast(I32))
+        nc.sync.dma_start(gs[1][64:128, :].bitcast(I32), gs[0][60:124, :].bitcast(I32))
         for e0, e1 in LOADS:
             load_words(0, e0, e1)
         for r, pos in enumerate((pos1, pos2)):
             nc.sync.dma_start(pos_t[r][:], pos)
-        nc.sync.dma_start(gate_t[:], gate.rearrange("r p t -> p r t"))
         for e0, e1 in LOADS:
             load_words(1, e0, e1)
         nc.sync.dma_start(w2w[:].bitcast(I32), w2_words[0].bitcast(I32))
@@ -99,14 +122,13 @@ def tile_moe_sdn_glu_relu_kernel(
         def gather_tokens(c0, c1):
             lst = offs_t[:, c0 // 16 : c1 // 16]
             for s in range(PASSES):
-                nc.vector.tensor_copy(gs[s][:, c0:c1], xs[:, s, :].indirect(lst))
-            for s in range(PASSES):
                 nc.vector.tensor_copy(gx[s][:, c0:c1], xw[s][:].bitcast(U32).indirect(lst))
 
         def unit(q, g, pair):
             e0, e1 = GROUPS[g]
             width = (e1 - e0) * C
-            sums = keep.tile([P, 2, width], F32, name=f"sums{q}_{g}")
+            direct = g == len(GROUPS) - 1
+            sums = keep.tile([P, 1 if direct else 2, width], F32, name=f"sums{q}_{g}")
             for m in range(2):
                 bank = banks[pair[m]]
                 cols = slice(P * (q % 2), P * (q % 2 + 1))
@@ -124,9 +146,10 @@ def tile_moe_sdn_glu_relu_kernel(
                         )
                 if m == 0:
                     nc.scalar.activation(sums[:, 0, :], bank[:, :width], RELU)
-                else:
+                elif not direct:
                     nc.scalar.copy(sums[:, 1, :], bank[:, :width])
-            nc.vector.tensor_tensor(h[q][:, e0 * C : e1 * C], sums[:, 0, :], sums[:, 1, :], MULT)
+            other = banks[pair[1]][:, :width] if direct else sums[:, 1, :]
+            nc.vector.tensor_tensor(h[q][:, e0 * C : e1 * C], other, sums[:, 0, :], MULT)
 
         def pick(q, t0, t1):
             y = keep.tile([P, 2, t1 - t0], F32, name=f"y{q}_{t0}")
@@ -136,7 +159,7 @@ def tile_moe_sdn_glu_relu_kernel(
                 )
             return y
 
-        def turn(q, t0, t1, y, into):
+        def turn(q, t0, t1, y, into, copy):
             for bank, j0 in zip(into, range(0, (t1 - t0) // P, 4)):
                 tiles = range(j0, min(j0 + 4, (t1 - t0) // P))
                 for j in tiles:
@@ -150,14 +173,14 @@ def tile_moe_sdn_glu_relu_kernel(
                             is_transpose=True,
                         )
                 for j in tiles:
-                    nc.scalar.copy(
+                    copy(
                         ct[t0 // P + j][:, :, 32 * q : 32 * (q + 1), :],
                         bank[:, (j - j0) * P : (j - j0 + 1) * P].rearrange("t (p u e) -> t u p e", u=2, e=2),
                     )
 
         out_v = out.rearrange("(a p) t -> p a t", p=P)
 
-        def turn_back(t0, t1, into):
+        def turn_back(t0, t1, into, copies):
             n = t1 - t0
             grouped = keep.tile([P, n, 4], BF16, name=f"grouped{t0}", align_bytes=64)
             for j in range(n // P):
@@ -165,12 +188,10 @@ def tile_moe_sdn_glu_relu_kernel(
                 back = into[j][:, : 2 * P]
                 for u in range(2):
                     nc.tensor.transpose(back[:, u * P : (u + 1) * P], pairs[:, u * P : (u + 1) * P], ident[:])
-                nc.scalar.copy(
-                    grouped[:, j * P : (j + 1) * P, :].bitcast(F32), back.rearrange("p (u t) -> p t u", u=2)
-                )
+                copies[j](grouped[:, j * P : (j + 1) * P, :].bitcast(F32), back.rearrange("p (u t) -> p t u", u=2))
             return grouped
 
-        def project(t0, t1, grouped, bank):
+        def project(t0, t1, grouped, bank, copy):
             n = t1 - t0
             codes = keep.tile([P, n], U32, name=f"codes{t0}", align_bytes=64)
             cs = keep.tile([P, n], U8, name=f"cs{t0}", align_bytes=64)
@@ -188,7 +209,7 @@ def tile_moe_sdn_glu_relu_kernel(
                     stop=True,
                 )
             res = keep.tile([P, 2, n], F32, name=f"res{t0}")
-            nc.vector.tensor_copy(res[:], bank[:, : 2 * n].rearrange("p (a t) -> p a t", a=2))
+            copy(res[:], bank[:, : 2 * n].rearrange("p (a t) -> p a t", a=2))
             nc.sync.dma_start(out_v[:, :, t0:t1], res[:])
 
         for c0, c1 in GATHERS:
@@ -208,13 +229,14 @@ def tile_moe_sdn_glu_relu_kernel(
         y2 = pick(2, 0, T)
         unit(3, 1, (4, 3))
         unit(3, 2, (0, 7))
-        turn(0, 0, T, y0, (banks[1], banks[4]))
-        turn(1, 0, T, y1, (banks[7], banks[0]))
-        turn(2, 0, T, y2, (banks[3], banks[4]))
+        by_scalar, by_vector = nc.scalar.copy, nc.vector.tensor_copy
+        turn(0, 0, T, y0, (banks[1], banks[4]), by_scalar)
+        turn(1, 0, T, y1, (banks[7], banks[0]), by_scalar)
+        turn(2, 0, T, y2, (banks[3], banks[4]), by_scalar)
         picked = [pick(HQ - 1, t0, t1) for t0, t1 in LAST_CHUNKS]
         made = []
         for i, (t0, t1) in enumerate(LAST_CHUNKS):
-            turn(HQ - 1, t0, t1, picked[i], [banks[(2, 5, 6)[i]]])
-            made.append(turn_back(t0, t1, [banks[b] for b in ((1, 7), (0, 3), (4,))[i]]))
+            turn(HQ - 1, t0, t1, picked[i], [banks[(2, 5, 6)[i]]], (by_scalar, by_scalar, by_vector)[i])
+            made.append(turn_back(t0, t1, [banks[b] for b in ((1, 7), (0, 3), (4,))[i]], ((by_scalar, by_scalar), (by_scalar, by_vector), (by_vector,))[i]))
         for i, (t0, t1) in enumerate(LAST_CHUNKS):
-            project(t0, t1, made[i], banks[(2, 5, 6)[i]])
+            project(t0, t1, made[i], banks[(2, 5, 6)[i]], (by_scalar, by_scalar, by_vector)[i])

@@ -23,8 +23,10 @@ S = E * C
 PASSES = K // 512
 HQ = H // P
 GROUPS = ((0, 4), (4, 8), (8, 10))
+GATE_ROWS = 8
+GATE_RUN = T // GATE_ROWS
 PLANE_EXPERTS = 5
-LOADS = ((0, 4), (4, 6), (6, 8), (8, 10))
+LOADS = GROUPS
 GATHERS = ((0, 256), (256, 512), (512, 896), (896, 1280))
 LAST_CHUNKS = ((0, 256), (256, 512), (512, 640))
 
@@ -41,7 +43,7 @@ def tile_moe_sdn_glu_relu_kernel(
         offs_t = keep.tile([P, S // 16], U16, name="offs_t")
         pos_t = [keep.tile([P, T // 16], U16, name=f"pos_t{r}") for r in range(2)]
         xw = [keep.tile([P, T], I32, name=f"xw{s}", align_bytes=64) for s in range(PASSES)]
-        xs = keep.tile([P, T], U8, name="xs", align_bytes=64)
+        xs = keep.tile([P, PASSES, T], U8, name="xs", align_bytes=64)
         w2w = keep.tile([P, 2 * N], U8, name="w2w", align_bytes=64)
         w2s = keep.tile([P, N], U8, name="w2s", align_bytes=64)
         gate_t = keep.tile([P, 2, T], F32, name="gate_t")
@@ -64,9 +66,9 @@ def tile_moe_sdn_glu_relu_kernel(
             for plane in pair:
                 nc.vector.memset(plane[:].bitcast(I32), 0)
         nc.gpsimd.memset(w2s[:].bitcast(I32), 0)
-        make_identity(nc, ident[:])
         gate_rows = keep.tile([P, P], F32, name="gate_rows")
         nc.gpsimd.memset(gate_rows[:], 0.0)
+        make_identity(nc, ident[:])
 
         def load_words(half, e0, e1):
             for m, src in enumerate((w1_words, w3_words)):
@@ -75,39 +77,18 @@ def tile_moe_sdn_glu_relu_kernel(
                 nc.sync.dma_start(dst.bitcast(I32), rows.bitcast(I32))
 
         nc.sync.dma_start(offs_t[:], offs)
-        for b in range(2):
-            nc.sync.dma_start(xs[32 * b : 32 * b + 8, :].bitcast(I32), x_scales[:, 4 * b : 4 * b + 4, :].bitcast(I32))
-        for b in range(2, 4):
-            for s in range(PASSES):
-                first = 32 * b - 4 * s
-                nc.sync.dma_start(xs[first : first + 4, :].bitcast(I32), x_scales[s, 4 * b : 4 * b + 4, :].bitcast(I32))
         for s in range(PASSES):
             nc.sync.dma_start(xw[s][:], x_words[s].rearrange("p t d -> p (t d)").bitcast(I32))
+        xs_rows = x_scales.rearrange("s (b r) t -> r b s t", r=4)
+        for r in range(4):
+            nc.sync.dma_start(xs[r:P:32, :, :].bitcast(I32), xs_rows[r].bitcast(I32))
+        nc.sync.dma_start(gate_rows[: 2 * GATE_ROWS, :GATE_RUN], gate[:, 0, :].rearrange("r (a t) -> r a t", t=GATE_RUN))
         for part, pair in enumerate(planes):
             for plane, src in zip(pair, (w1_scales, w3_scales)):
                 some = src[part * PLANE_EXPERTS : (part + 1) * PLANE_EXPERTS]
                 rows = some.rearrange("e s (b r) i -> r b (e s) i", r=4)
                 for r in range(4):
                     nc.sync.dma_start(plane[r:P:32, :, :].bitcast(I32), rows[r].bitcast(I32))
-        for r in range(2):
-            nc.sync.dma_start(gate_rows[4 * r : 4 * r + 4, :], gate[r, 0, :BANK].rearrange("(j t) -> j t", t=P))
-        nc.sync.dma_start(gate_rows[8:10, :], gate[:, 0, BANK:])
-        nc.tensor.transpose(banks[7][:, :P], gate_rows[:], ident[:])
-        gate_cols = keep.tile([P, 16], F32, name="gate_cols")
-        nc.scalar.copy(gate_cols[:], banks[7][:, :16])
-        for b, count in ((4, 4), (5, 4), (6, 2)):
-            for j in range(count):
-                c = 4 * (b - 4) + j
-                nc.tensor.transpose(
-                    banks[b][:, j * P : (j + 1) * P], gate_cols[:, c : c + 1].to_broadcast([P, P]), ident[:]
-                )
-        for r in range(2):
-            nc.scalar.copy(gate_t[:, r, :BANK], banks[4 + r][:])
-        nc.scalar.copy(gate_t[:, :, BANK:], banks[6][:, : 2 * P].rearrange("p (r t) -> p r t", r=2))
-        for c0, c1 in GATHERS:
-            nc.vector.tensor_copy(gs[0][:, c0:c1], xs[:].indirect(offs_t[:, c0 // 16 : c1 // 16]))
-        nc.sync.dma_start(gs[1][0:64, :].bitcast(I32), gs[0][4:68, :].bitcast(I32))
-        nc.sync.dma_start(gs[1][64:128, :].bitcast(I32), gs[0][60:124, :].bitcast(I32))
         for e0, e1 in LOADS:
             load_words(0, e0, e1)
         for r, pos in enumerate((pos1, pos2)):
@@ -119,8 +100,21 @@ def tile_moe_sdn_glu_relu_kernel(
         for r in range(4):
             nc.sync.dma_start(w2s[r:P:32, :].bitcast(I32), w2_rows[r].bitcast(I32))
 
+        nc.tensor.transpose(banks[0][:, :P], gate_rows[:], ident[:])
+        gate_cols = keep.tile([P, 2 * GATE_ROWS], F32, name="gate_cols")
+        nc.scalar.copy(gate_cols[:], banks[0][:, : 2 * GATE_ROWS])
+        gate_runs = gate_t[:].rearrange("p r (a t) -> p (r a) t", t=GATE_RUN)
+        for c0 in range(0, 2 * GATE_ROWS, 4):
+            bank = banks[4 + c0 // 4]
+            for j in range(4):
+                column = gate_cols[:, c0 + j : c0 + j + 1]
+                nc.tensor.transpose(bank[:, j * P : (j + 1) * P], column.to_broadcast([P, P]), ident[:])
+            nc.scalar.copy(gate_runs[:, c0 : c0 + 4, :], bank[:].rearrange("p (j t) -> p j t", t=P)[:, :, :GATE_RUN])
+
         def gather_tokens(c0, c1):
             lst = offs_t[:, c0 // 16 : c1 // 16]
+            for s in range(PASSES):
+                nc.vector.tensor_copy(gs[s][:, c0:c1], xs[:, s, :].indirect(lst))
             for s in range(PASSES):
                 nc.vector.tensor_copy(gx[s][:, c0:c1], xw[s][:].bitcast(U32).indirect(lst))
 
@@ -230,9 +224,9 @@ def tile_moe_sdn_glu_relu_kernel(
         unit(3, 1, (4, 3))
         unit(3, 2, (0, 7))
         by_scalar, by_vector = nc.scalar.copy, nc.vector.tensor_copy
-        turn(0, 0, T, y0, (banks[1], banks[4]), by_scalar)
-        turn(1, 0, T, y1, (banks[7], banks[0]), by_scalar)
-        turn(2, 0, T, y2, (banks[3], banks[4]), by_scalar)
+        turn(0, 0, T, y0, (banks[4], banks[4]), by_scalar)
+        turn(1, 0, T, y1, (banks[0], banks[0]), by_scalar)
+        turn(2, 0, T, y2, (banks[3], banks[6]), by_scalar)
         picked = [pick(HQ - 1, t0, t1) for t0, t1 in LAST_CHUNKS]
         made = []
         for i, (t0, t1) in enumerate(LAST_CHUNKS):

@@ -25,10 +25,8 @@ HQ = H // P
 GROUPS = ((0, 4), (4, 8), (8, 10))
 GATE_ROWS = 8
 GATE_RUN = T // GATE_ROWS
-PLANE_EXPERTS = 5
-LOADS = GROUPS
-GATHERS = ((0, 256), (256, 512), (512, 896), (896, 1280))
-LAST_CHUNKS = ((0, 256), (256, 512), (512, 640))
+GATHER_RUN = 256
+CHUNKS = ((0, 256), (256, 384), (384, 512), (512, 640))
 
 
 def tile_moe_sdn_glu_relu_kernel(
@@ -51,15 +49,12 @@ def tile_moe_sdn_glu_relu_kernel(
         gx = [keep.tile([P, S], U32, name=f"gx{s}", align_bytes=64) for s in range(PASSES)]
         gs = [keep.tile([P, S], U8, name=f"gs{s}", align_bytes=64) for s in range(PASSES)]
         h = [keep.tile([P, S], F32, name=f"h{q}") for q in range(HQ)]
-        ct = [keep.tile([P, 2, P, 2], BF16, name=f"ct{j}", align_bytes=64) for j in range(T // P)]
+        ct = [keep.tile([P, (t1 - t0) // P, 2, P, 2], BF16, name=f"ct{t0}", align_bytes=64) for t0, t1 in CHUNKS]
         planes = [
-            [keep.tile([P, PLANE_EXPERTS * PASSES, H], U8, name=f"plane{part}_{m}", align_bytes=64) for m in range(2)]
-            for part in range(E // PLANE_EXPERTS)
+            [keep.tile([P, (e1 - e0) * PASSES, H], U8, name=f"plane{e0}_{m}", align_bytes=64) for m in range(2)]
+            for e0, e1 in GROUPS
         ]
-        words = [
-            [keep.tile([P, E * PASSES, 4 * P], U8, name=f"words{half}_{m}", align_bytes=64) for m in range(2)]
-            for half in range(2)
-        ]
+        words = {}
 
         nc.gpsimd.memset(xs[:].bitcast(I32), 0)
         for pair in planes:
@@ -70,11 +65,18 @@ def tile_moe_sdn_glu_relu_kernel(
         nc.gpsimd.memset(gate_rows[:], 0.0)
         make_identity(nc, ident[:])
 
-        def load_words(half, e0, e1):
-            for m, src in enumerate((w1_words, w3_words)):
-                rows = src[e0:e1].rearrange("e s p b -> p (e s) b")[:, :, 4 * P * half : 4 * P * (half + 1)]
-                dst = words[half][m][:, e0 * PASSES : e1 * PASSES, :]
-                nc.sync.dma_start(dst.bitcast(I32), rows.bitcast(I32))
+        def load_words(half, groups, tags):
+            first, end = GROUPS[groups[0]][0], GROUPS[groups[-1]][1]
+            pair = [
+                keep.tile([P, (end - first) * PASSES, 4 * P], U8, name=f"words{half}_{first}_{m}", tag=tags[m], align_bytes=64)
+                for m in range(2)
+            ]
+            for g in groups:
+                e0, e1 = GROUPS[g]
+                for m, src in enumerate((w1_words, w3_words)):
+                    rows = src[e0:e1].rearrange("e s p b -> p (e s) b")[:, :, 4 * P * half : 4 * P * (half + 1)]
+                    words[half, g, m] = pair[m][:, (e0 - first) * PASSES : (e1 - first) * PASSES, :]
+                    nc.sync.dma_start(words[half, g, m].bitcast(I32), rows.bitcast(I32))
 
         nc.sync.dma_start(offs_t[:], offs)
         for s in range(PASSES):
@@ -82,47 +84,46 @@ def tile_moe_sdn_glu_relu_kernel(
         xs_rows = x_scales.rearrange("s (b r) t -> r b s t", r=4)
         for r in range(4):
             nc.sync.dma_start(xs[r:P:32, :, :].bitcast(I32), xs_rows[r].bitcast(I32))
+        load_words(0, (0, 1), ("early0", "early1"))
         nc.sync.dma_start(gate_rows[: 2 * GATE_ROWS, :GATE_RUN], gate[:, 0, :].rearrange("r (a t) -> r a t", t=GATE_RUN))
-        for part, pair in enumerate(planes):
-            for plane, src in zip(pair, (w1_scales, w3_scales)):
-                some = src[part * PLANE_EXPERTS : (part + 1) * PLANE_EXPERTS]
-                rows = some.rearrange("e s (b r) i -> r b (e s) i", r=4)
-                for r in range(4):
-                    nc.sync.dma_start(plane[r:P:32, :, :].bitcast(I32), rows[r].bitcast(I32))
-        for e0, e1 in LOADS:
-            load_words(0, e0, e1)
         for r, pos in enumerate((pos1, pos2)):
             nc.sync.dma_start(pos_t[r][:], pos)
-        for e0, e1 in LOADS:
-            load_words(1, e0, e1)
+        for (e0, e1), pair in zip(GROUPS, planes):
+            for plane, src in zip(pair, (w1_scales, w3_scales)):
+                rows = src[e0:e1].rearrange("e s (b r) i -> r b (e s) i", r=4)
+                for r in range(4):
+                    nc.sync.dma_start(plane[r:P:32, :, :].bitcast(I32), rows[r].bitcast(I32))
         nc.sync.dma_start(w2w[:].bitcast(I32), w2_words[0].bitcast(I32))
         w2_rows = w2_scales[0].rearrange("(b r) n -> r b n", r=4)
         for r in range(4):
             nc.sync.dma_start(w2s[r:P:32, :].bitcast(I32), w2_rows[r].bitcast(I32))
 
         nc.tensor.transpose(banks[0][:, :P], gate_rows[:], ident[:])
-        gate_cols = keep.tile([P, 2 * GATE_ROWS], F32, name="gate_cols")
-        nc.scalar.copy(gate_cols[:], banks[0][:, : 2 * GATE_ROWS])
         gate_runs = gate_t[:].rearrange("p r (a t) -> p (r a) t", t=GATE_RUN)
         for c0 in range(0, 2 * GATE_ROWS, 4):
+            gate_cols = keep.tile([P, 4], F32, name=f"gate_cols{c0}", tag=f"late{c0 // 4}", align_bytes=64)
+            nc.scalar.copy(gate_cols[:], banks[0][:, c0 : c0 + 4])
             bank = banks[4 + c0 // 4]
             for j in range(4):
-                column = gate_cols[:, c0 + j : c0 + j + 1]
+                column = gate_cols[:, j : j + 1]
                 nc.tensor.transpose(bank[:, j * P : (j + 1) * P], column.to_broadcast([P, P]), ident[:])
             nc.scalar.copy(gate_runs[:, c0 : c0 + 4, :], bank[:].rearrange("p (j t) -> p j t", t=P)[:, :, :GATE_RUN])
+
+        load_words(0, (2,), ("late0", "late1"))
+        load_words(1, (0, 1, 2), ("late2", "late3"))
 
         def gather_tokens(c0, c1):
             lst = offs_t[:, c0 // 16 : c1 // 16]
             for s in range(PASSES):
-                nc.vector.tensor_copy(gs[s][:, c0:c1], xs[:, s, :].indirect(lst))
-            for s in range(PASSES):
                 nc.vector.tensor_copy(gx[s][:, c0:c1], xw[s][:].bitcast(U32).indirect(lst))
+            for s in range(PASSES):
+                nc.vector.tensor_copy(gs[s][:, c0:c1], xs[:, s, :].indirect(lst))
 
         def unit(q, g, pair):
             e0, e1 = GROUPS[g]
             width = (e1 - e0) * C
             direct = g == len(GROUPS) - 1
-            sums = keep.tile([P, 1 if direct else 2, width], F32, name=f"sums{q}_{g}")
+            sums = keep.tile([P, 1 if direct else 2, width], F32, name=f"sums{q}_{g}", align_bytes=64)
             for m in range(2):
                 bank = banks[pair[m]]
                 cols = slice(P * (q % 2), P * (q % 2 + 1))
@@ -131,8 +132,8 @@ def tile_moe_sdn_glu_relu_kernel(
                     for s in range(PASSES):
                         nc.tensor.matmul_mx(
                             out=bank[:, (e - e0) * C : (e - e0 + 1) * C],
-                            lhsT=words[q // 2][m][:, e * PASSES + s, 2 * cols.start : 2 * cols.stop].bitcast(FP4X4),
-                            lhsT_scale=planes[e // PLANE_EXPERTS][m][:, e % PLANE_EXPERTS * PASSES + s, P * q : P * (q + 1)],
+                            lhsT=words[q // 2, g, m][:, (e - e0) * PASSES + s, 2 * cols.start : 2 * cols.stop].bitcast(FP4X4),
+                            lhsT_scale=planes[g][m][:, (e - e0) * PASSES + s, P * q : P * (q + 1)],
                             rhs=gx[s][:, slots].bitcast(FP8X4),
                             rhs_scale=gs[s][:, slots],
                             start=(s == 0),
@@ -144,45 +145,48 @@ def tile_moe_sdn_glu_relu_kernel(
                     nc.scalar.copy(sums[:, 1, :], bank[:, :width])
             other = banks[pair[1]][:, :width] if direct else sums[:, 1, :]
             nc.vector.tensor_tensor(h[q][:, e0 * C : e1 * C], other, sums[:, 0, :], MULT)
+            return sums
 
-        def pick(q, t0, t1):
-            y = keep.tile([P, 2, t1 - t0], F32, name=f"y{q}_{t0}")
+        def pick(q, t0, t1, y=None):
+            if y is None:
+                y = keep.tile([P, 2, t1 - t0], F32, name=f"y{q}_{t0}")[:]
             for r in range(2):
                 nc.vector.tensor_tensor(
                     y[:, r, :], h[q][:].indirect(pos_t[r][:, t0 // 16 : t1 // 16]), gate_t[:, r, t0:t1], MULT
                 )
             return y
 
-        def turn(q, t0, t1, y, into, copy):
-            for bank, j0 in zip(into, range(0, (t1 - t0) // P, 4)):
-                tiles = range(j0, min(j0 + 4, (t1 - t0) // P))
-                for j in tiles:
+        def turn(half, c, ys, into, copy):
+            tiles = (CHUNKS[c][1] - CHUNKS[c][0]) // P
+            for qq in range(2):
+                for j in range(tiles):
                     for r in range(2):
                         nc.tensor.matmul(
-                            bank[:, (j - j0) * P : (j - j0 + 1) * P],
-                            lhsT=y[:, r, j * P : (j + 1) * P],
+                            into[:, (2 * j + qq) * P : (2 * j + qq + 1) * P],
+                            lhsT=ys[qq][:, r, j * P : (j + 1) * P],
                             rhs=ident[:],
                             start=(r == 0),
                             stop=(r == 1),
                             is_transpose=True,
                         )
-                for j in tiles:
-                    copy(
-                        ct[t0 // P + j][:, :, 32 * q : 32 * (q + 1), :],
-                        bank[:, (j - j0) * P : (j - j0 + 1) * P].rearrange("t (p u e) -> t u p e", u=2, e=2),
-                    )
+            return lambda: copy(
+                ct[c][:, :, :, 64 * half : 64 * (half + 1), :],
+                into.rearrange("t (j p u e) -> t j u p e", p=64, u=2, e=2),
+            )
 
         out_v = out.rearrange("(a p) t -> p a t", p=P)
 
-        def turn_back(t0, t1, into, copies):
+        def turn_back(c, bank, copy):
+            t0, t1 = CHUNKS[c]
             n = t1 - t0
             grouped = keep.tile([P, n, 4], BF16, name=f"grouped{t0}", align_bytes=64)
-            for j in range(n // P):
-                pairs = ct[t0 // P + j][:].rearrange("t u p e -> t (u p e)").bitcast(F32)
-                back = into[j][:, : 2 * P]
-                for u in range(2):
-                    nc.tensor.transpose(back[:, u * P : (u + 1) * P], pairs[:, u * P : (u + 1) * P], ident[:])
-                copies[j](grouped[:, j * P : (j + 1) * P, :].bitcast(F32), back.rearrange("p (u t) -> p t u", u=2))
+            pairs = ct[c][:].rearrange("t j u p e -> t (j u p e)").bitcast(F32)
+            for b in range(2 * n // P):
+                nc.tensor.transpose(bank[:, b * P : (b + 1) * P], pairs[:, b * P : (b + 1) * P], ident[:])
+            copy(
+                grouped[:].bitcast(F32).rearrange("p (j t) u -> p j t u", t=P),
+                bank[:, : 2 * n].rearrange("p (j u t) -> p j t u", u=2, t=P),
+            )
             return grouped
 
         def project(t0, t1, grouped, bank, copy):
@@ -206,31 +210,42 @@ def tile_moe_sdn_glu_relu_kernel(
             copy(res[:], bank[:, : 2 * n].rearrange("p (a t) -> p a t", a=2))
             nc.sync.dma_start(out_v[:, :, t0:t1], res[:])
 
-        for c0, c1 in GATHERS:
-            gather_tokens(c0, c1)
+        for c0 in range(0, S, GATHER_RUN):
+            gather_tokens(c0, c0 + GATHER_RUN)
         unit(0, 0, (0, 1))
         unit(1, 0, (2, 3))
         unit(0, 1, (4, 5))
+        unit(1, 1, (6, 7))
         unit(0, 2, (0, 1))
         y0 = pick(0, 0, T)
-        unit(1, 1, (0, 3))
-        unit(1, 2, (2, 5))
+        unit(1, 2, (2, 3))
         y1 = pick(1, 0, T)
-        unit(2, 0, (4, 1))
-        unit(3, 0, (0, 3))
-        unit(2, 1, (6, 7))
-        unit(2, 2, (4, 1))
-        y2 = pick(2, 0, T)
-        unit(3, 1, (4, 3))
-        unit(3, 2, (0, 7))
+        unit(2, 0, (4, 5))
+        unit(3, 0, (6, 7))
+        unit(2, 1, (0, 1))
+        unit(2, 2, (2, 3))
+        y2 = [pick(2, *CHUNKS[0])]
+        unit(3, 2, (6, 7))
+        spent = unit(3, 1, (2, 4))
         by_scalar, by_vector = nc.scalar.copy, nc.vector.tensor_copy
-        turn(0, 0, T, y0, (banks[4], banks[4]), by_scalar)
-        turn(1, 0, T, y1, (banks[0], banks[0]), by_scalar)
-        turn(2, 0, T, y2, (banks[3], banks[6]), by_scalar)
-        picked = [pick(HQ - 1, t0, t1) for t0, t1 in LAST_CHUNKS]
-        made = []
-        for i, (t0, t1) in enumerate(LAST_CHUNKS):
-            turn(HQ - 1, t0, t1, picked[i], [banks[(2, 5, 6)[i]]], (by_scalar, by_scalar, by_vector)[i])
-            made.append(turn_back(t0, t1, [banks[b] for b in ((1, 7), (0, 3), (4,))[i]], ((by_scalar, by_scalar), (by_scalar, by_vector), (by_vector,))[i]))
-        for i, (t0, t1) in enumerate(LAST_CHUNKS):
-            project(t0, t1, made[i], banks[(2, 5, 6)[i]], (by_scalar, by_scalar, by_vector)[i])
+        early = ((banks[2], (0,)), (banks[4], (1, 2)), (banks[2], (3,)))
+        for bank, chunks in early:
+            copies = []
+            for place, c in enumerate(chunks):
+                t0, t1 = CHUNKS[c]
+                width = 2 * (t1 - t0)
+                ys = [y[:, :, t0:t1] for y in (y0, y1)]
+                copies.append(turn(0, c, ys, bank[:, place * width : (place + 1) * width], by_scalar))
+            for copy in copies:
+                copy()
+        room = spent[:].rearrange("p m (a t) -> p (m a) t", t=P)
+        last = len(CHUNKS) - 1
+        for c, (t0, t1) in enumerate(CHUNKS):
+            if c > 0:
+                y2.append(pick(2, t0, t1, room[:, 2 * (c - 1) : 2 * c, :]))
+            y3 = pick(3, t0, t1)
+            ring = (0, 1, 3) if c % 2 == 0 else (5, 6, 7)
+            edge = by_vector if c == last else by_scalar
+            turn(1, c, (y2[c], y3), banks[ring[0]][:, : 2 * (t1 - t0)], edge)()
+            grouped = turn_back(c, banks[ring[1]], by_scalar)
+            project(t0, t1, grouped, banks[ring[2]], edge)

@@ -25,7 +25,8 @@ HQ = H // P
 GROUPS = ((0, 4), (4, 8), (8, 10))
 GATE_ROWS = 8
 GATE_RUN = T // GATE_ROWS
-GATHER_RUN = 256
+SCALE_LOADS = ((0, 4), (4, 10))
+GATHERS = ((0, 256), (256, 512), (512, 896), (896, 1280))
 CHUNKS = ((0, 256), (256, 384), (384, 512), (512, 640))
 
 
@@ -52,18 +53,19 @@ def tile_moe_sdn_glu_relu_kernel(
         ct = [keep.tile([P, (t1 - t0) // P, 2, P, 2], BF16, name=f"ct{t0}", align_bytes=64) for t0, t1 in CHUNKS]
         planes = [
             [keep.tile([P, (e1 - e0) * PASSES, H], U8, name=f"plane{e0}_{m}", align_bytes=64) for m in range(2)]
-            for e0, e1 in GROUPS
+            for e0, e1 in SCALE_LOADS
         ]
         words = {}
 
         nc.gpsimd.memset(xs[:].bitcast(I32), 0)
-        for pair in planes:
-            for plane in pair:
-                nc.vector.memset(plane[:].bitcast(I32), 0)
+        nc.vector.memset(planes[0][0][:].bitcast(I32), 0)
+        nc.gpsimd.memset(planes[0][1][:].bitcast(I32), 0)
+        nc.vector.memset(planes[1][0][:].bitcast(I32), 0)
         nc.gpsimd.memset(w2s[:].bitcast(I32), 0)
         gate_rows = keep.tile([P, P], F32, name="gate_rows")
         nc.gpsimd.memset(gate_rows[:], 0.0)
         make_identity(nc, ident[:])
+        nc.gpsimd.memset(planes[1][1][:].bitcast(I32), 0)
 
         def load_words(half, groups, tags):
             first, end = GROUPS[groups[0]][0], GROUPS[groups[-1]][1]
@@ -84,11 +86,11 @@ def tile_moe_sdn_glu_relu_kernel(
         xs_rows = x_scales.rearrange("s (b r) t -> r b s t", r=4)
         for r in range(4):
             nc.sync.dma_start(xs[r:P:32, :, :].bitcast(I32), xs_rows[r].bitcast(I32))
-        load_words(0, (0, 1), ("early0", "early1"))
         nc.sync.dma_start(gate_rows[: 2 * GATE_ROWS, :GATE_RUN], gate[:, 0, :].rearrange("r (a t) -> r a t", t=GATE_RUN))
+        load_words(0, (0, 1), ("early0", "early1"))
         for r, pos in enumerate((pos1, pos2)):
             nc.sync.dma_start(pos_t[r][:], pos)
-        for (e0, e1), pair in zip(GROUPS, planes):
+        for (e0, e1), pair in zip(SCALE_LOADS, planes):
             for plane, src in zip(pair, (w1_scales, w3_scales)):
                 rows = src[e0:e1].rearrange("e s (b r) i -> r b (e s) i", r=4)
                 for r in range(4):
@@ -133,7 +135,7 @@ def tile_moe_sdn_glu_relu_kernel(
                         nc.tensor.matmul_mx(
                             out=bank[:, (e - e0) * C : (e - e0 + 1) * C],
                             lhsT=words[q // 2, g, m][:, (e - e0) * PASSES + s, 2 * cols.start : 2 * cols.stop].bitcast(FP4X4),
-                            lhsT_scale=planes[g][m][:, (e - e0) * PASSES + s, P * q : P * (q + 1)],
+                            lhsT_scale=planes[min(g, 1)][m][:, (e - SCALE_LOADS[min(g, 1)][0]) * PASSES + s, P * q : P * (q + 1)],
                             rhs=gx[s][:, slots].bitcast(FP8X4),
                             rhs_scale=gs[s][:, slots],
                             start=(s == 0),
@@ -210,8 +212,8 @@ def tile_moe_sdn_glu_relu_kernel(
             copy(res[:], bank[:, : 2 * n].rearrange("p (a t) -> p a t", a=2))
             nc.sync.dma_start(out_v[:, :, t0:t1], res[:])
 
-        for c0 in range(0, S, GATHER_RUN):
-            gather_tokens(c0, c0 + GATHER_RUN)
+        for c0, c1 in GATHERS:
+            gather_tokens(c0, c1)
         unit(0, 0, (0, 1))
         unit(1, 0, (2, 3))
         unit(0, 1, (4, 5))

@@ -61,11 +61,11 @@ def tile_moe_sdn_glu_relu_kernel(
         nc.vector.memset(planes[0][0][:].bitcast(I32), 0)
         nc.gpsimd.memset(planes[0][1][:].bitcast(I32), 0)
         nc.vector.memset(planes[1][0][:].bitcast(I32), 0)
-        nc.gpsimd.memset(w2s[:].bitcast(I32), 0)
         gate_rows = keep.tile([P, P], F32, name="gate_rows")
         nc.gpsimd.memset(gate_rows[:], 0.0)
-        make_identity(nc, ident[:])
         nc.gpsimd.memset(planes[1][1][:].bitcast(I32), 0)
+        make_identity(nc, ident[:])
+        nc.gpsimd.memset(w2s[:].bitcast(I32), 0)
 
         def load_words(half, groups, tags):
             first, end = GROUPS[groups[0]][0], GROUPS[groups[-1]][1]
@@ -88,22 +88,16 @@ def tile_moe_sdn_glu_relu_kernel(
             nc.sync.dma_start(xs[r:P:32, :, :].bitcast(I32), xs_rows[r].bitcast(I32))
         nc.sync.dma_start(gate_rows[: 2 * GATE_ROWS, :GATE_RUN], gate[:, 0, :].rearrange("r (a t) -> r a t", t=GATE_RUN))
         load_words(0, (0, 1), ("early0", "early1"))
-        for r, pos in enumerate((pos1, pos2)):
-            nc.sync.dma_start(pos_t[r][:], pos)
         for (e0, e1), pair in zip(SCALE_LOADS, planes):
             for plane, src in zip(pair, (w1_scales, w3_scales)):
                 rows = src[e0:e1].rearrange("e s (b r) i -> r b (e s) i", r=4)
                 for r in range(4):
                     nc.sync.dma_start(plane[r:P:32, :, :].bitcast(I32), rows[r].bitcast(I32))
-        nc.sync.dma_start(w2w[:].bitcast(I32), w2_words[0].bitcast(I32))
-        w2_rows = w2_scales[0].rearrange("(b r) n -> r b n", r=4)
-        for r in range(4):
-            nc.sync.dma_start(w2s[r:P:32, :].bitcast(I32), w2_rows[r].bitcast(I32))
 
         nc.tensor.transpose(banks[0][:, :P], gate_rows[:], ident[:])
         gate_runs = gate_t[:].rearrange("p r (a t) -> p (r a) t", t=GATE_RUN)
         for c0 in range(0, 2 * GATE_ROWS, 4):
-            gate_cols = keep.tile([P, 4], F32, name=f"gate_cols{c0}", tag=f"late{c0 // 4}", align_bytes=64)
+            gate_cols = keep.tile([P, 4], F32, name=f"gate_cols{c0}")
             nc.scalar.copy(gate_cols[:], banks[0][:, c0 : c0 + 4])
             bank = banks[4 + c0 // 4]
             for j in range(4):
@@ -112,7 +106,14 @@ def tile_moe_sdn_glu_relu_kernel(
             nc.scalar.copy(gate_runs[:, c0 : c0 + 4, :], bank[:].rearrange("p (j t) -> p j t", t=P)[:, :, :GATE_RUN])
 
         load_words(0, (2,), ("late0", "late1"))
-        load_words(1, (0, 1, 2), ("late2", "late3"))
+        load_words(1, (0,), ("late2", "late3"))
+        for r, pos in enumerate((pos1, pos2)):
+            nc.sync.dma_start(pos_t[r][:], pos)
+        load_words(1, (1, 2), ("late4", "late5"))
+        nc.sync.dma_start(w2w[:].bitcast(I32), w2_words[0].bitcast(I32))
+        w2_rows = w2_scales[0].rearrange("(b r) n -> r b n", r=4)
+        for r in range(4):
+            nc.sync.dma_start(w2s[r:P:32, :].bitcast(I32), w2_rows[r].bitcast(I32))
 
         def gather_tokens(c0, c1):
             lst = offs_t[:, c0 // 16 : c1 // 16]
@@ -225,12 +226,12 @@ def tile_moe_sdn_glu_relu_kernel(
         unit(2, 0, (4, 5))
         unit(3, 0, (6, 7))
         unit(2, 1, (0, 1))
-        unit(2, 2, (2, 3))
+        unit(3, 1, (2, 3))
+        unit(2, 2, (4, 5))
         y2 = [pick(2, *CHUNKS[0])]
         unit(3, 2, (6, 7))
-        spent = unit(3, 1, (2, 4))
         by_scalar, by_vector = nc.scalar.copy, nc.vector.tensor_copy
-        early = ((banks[2], (0,)), (banks[4], (1, 2)), (banks[2], (3,)))
+        early = ((banks[4], (0,)), (banks[6], (1, 2)), (banks[4], (3,)))
         for bank, chunks in early:
             copies = []
             for place, c in enumerate(chunks):
@@ -240,13 +241,12 @@ def tile_moe_sdn_glu_relu_kernel(
                 copies.append(turn(0, c, ys, bank[:, place * width : (place + 1) * width], by_scalar))
             for copy in copies:
                 copy()
-        room = spent[:].rearrange("p m (a t) -> p (m a) t", t=P)
         last = len(CHUNKS) - 1
         for c, (t0, t1) in enumerate(CHUNKS):
             if c > 0:
-                y2.append(pick(2, t0, t1, room[:, 2 * (c - 1) : 2 * c, :]))
+                y2.append(pick(2, t0, t1))
             y3 = pick(3, t0, t1)
-            ring = (0, 1, 3) if c % 2 == 0 else (5, 6, 7)
+            ring = (0, 1, 2) if c % 2 == 0 else (3, 5, 7)
             edge = by_vector if c == last else by_scalar
             turn(1, c, (y2[c], y3), banks[ring[0]][:, : 2 * (t1 - t0)], edge)()
             grouped = turn_back(c, banks[ring[1]], by_scalar)

@@ -25,8 +25,7 @@ HQ = H // P
 GROUPS = ((0, 4), (4, 8), (8, 10))
 GATE_ROWS = 8
 GATE_RUN = T // GATE_ROWS
-SCALE_LOADS = ((0, 4), (4, 10))
-GATHERS = ((0, 256), (256, 512), (512, 896), (896, 1280))
+GATHERS = ((0, 384), (384, 768), (768, 1024), (1024, 1280))
 CHUNKS = ((0, 256), (256, 384), (384, 512), (512, 640))
 
 
@@ -52,33 +51,35 @@ def tile_moe_sdn_glu_relu_kernel(
         h = [keep.tile([P, S], F32, name=f"h{q}") for q in range(HQ)]
         ct = [keep.tile([P, (t1 - t0) // P, 2, P, 2], BF16, name=f"ct{t0}", align_bytes=64) for t0, t1 in CHUNKS]
         planes = [
-            [keep.tile([P, (e1 - e0) * PASSES, H], U8, name=f"plane{e0}_{m}", align_bytes=64) for m in range(2)]
-            for e0, e1 in SCALE_LOADS
+            [keep.tile([P, E * PASSES, 2 * P], U8, name=f"plane{half}_{m}", align_bytes=64) for m in range(2)]
+            for half in range(2)
         ]
         words = {}
 
         nc.gpsimd.memset(xs[:].bitcast(I32), 0)
         nc.vector.memset(planes[0][0][:].bitcast(I32), 0)
-        nc.gpsimd.memset(planes[0][1][:].bitcast(I32), 0)
-        nc.vector.memset(planes[1][0][:].bitcast(I32), 0)
         gate_rows = keep.tile([P, P], F32, name="gate_rows")
         nc.gpsimd.memset(gate_rows[:], 0.0)
-        nc.gpsimd.memset(planes[1][1][:].bitcast(I32), 0)
+        nc.gpsimd.memset(planes[0][1][:].bitcast(I32), 0)
         make_identity(nc, ident[:])
+        nc.gpsimd.memset(planes[1][0][:].bitcast(I32), 0)
+        nc.gpsimd.memset(planes[1][1][:].bitcast(I32), 0)
         nc.gpsimd.memset(w2s[:].bitcast(I32), 0)
 
-        def load_words(half, groups, tags):
-            first, end = GROUPS[groups[0]][0], GROUPS[groups[-1]][1]
-            pair = [
-                keep.tile([P, (end - first) * PASSES, 4 * P], U8, name=f"words{half}_{first}_{m}", tag=tags[m], align_bytes=64)
-                for m in range(2)
-            ]
-            for g in groups:
-                e0, e1 = GROUPS[g]
-                for m, src in enumerate((w1_words, w3_words)):
-                    rows = src[e0:e1].rearrange("e s p b -> p (e s) b")[:, :, 4 * P * half : 4 * P * (half + 1)]
-                    words[half, g, m] = pair[m][:, (e0 - first) * PASSES : (e1 - first) * PASSES, :]
-                    nc.sync.dma_start(words[half, g, m].bitcast(I32), rows.bitcast(I32))
+        def load_words(half, g):
+            e0, e1 = GROUPS[g]
+            for m, src in enumerate((w1_words, w3_words)):
+                rows = src[e0:e1].rearrange("e s p b -> p (e s) b")[:, :, 4 * P * half : 4 * P * (half + 1)]
+                tile = keep.tile([P, (e1 - e0) * PASSES, 4 * P], U8, name=f"words{half}_{g}_{m}", align_bytes=64)
+                words[half, g, m] = tile
+                nc.sync.dma_start(tile[:].bitcast(I32), rows.bitcast(I32))
+
+        def load_scales(half):
+            for plane, src in zip(planes[half], (w1_scales, w3_scales)):
+                rows = src.rearrange("e s (b r) i -> r b (e s) i", r=4)
+                for r in range(4):
+                    part = rows[r][:, :, 2 * P * half : 2 * P * (half + 1)]
+                    nc.sync.dma_start(plane[r:P:32, :, :].bitcast(I32), part.bitcast(I32))
 
         nc.sync.dma_start(offs_t[:], offs)
         for s in range(PASSES):
@@ -87,12 +88,12 @@ def tile_moe_sdn_glu_relu_kernel(
         for r in range(4):
             nc.sync.dma_start(xs[r:P:32, :, :].bitcast(I32), xs_rows[r].bitcast(I32))
         nc.sync.dma_start(gate_rows[: 2 * GATE_ROWS, :GATE_RUN], gate[:, 0, :].rearrange("r (a t) -> r a t", t=GATE_RUN))
-        load_words(0, (0, 1), ("early0", "early1"))
-        for (e0, e1), pair in zip(SCALE_LOADS, planes):
-            for plane, src in zip(pair, (w1_scales, w3_scales)):
-                rows = src[e0:e1].rearrange("e s (b r) i -> r b (e s) i", r=4)
-                for r in range(4):
-                    nc.sync.dma_start(plane[r:P:32, :, :].bitcast(I32), rows[r].bitcast(I32))
+        load_scales(0)
+        for g in range(len(GROUPS)):
+            load_words(0, g)
+        for r, pos in enumerate((pos1, pos2)):
+            nc.sync.dma_start(pos_t[r][:], pos)
+        load_scales(1)
 
         nc.tensor.transpose(banks[0][:, :P], gate_rows[:], ident[:])
         gate_runs = gate_t[:].rearrange("p r (a t) -> p (r a) t", t=GATE_RUN)
@@ -105,11 +106,8 @@ def tile_moe_sdn_glu_relu_kernel(
                 nc.tensor.transpose(bank[:, j * P : (j + 1) * P], column.to_broadcast([P, P]), ident[:])
             nc.scalar.copy(gate_runs[:, c0 : c0 + 4, :], bank[:].rearrange("p (j t) -> p j t", t=P)[:, :, :GATE_RUN])
 
-        load_words(0, (2,), ("late0", "late1"))
-        load_words(1, (0,), ("late2", "late3"))
-        for r, pos in enumerate((pos1, pos2)):
-            nc.sync.dma_start(pos_t[r][:], pos)
-        load_words(1, (1, 2), ("late4", "late5"))
+        for g in range(len(GROUPS)):
+            load_words(1, g)
         nc.sync.dma_start(w2w[:].bitcast(I32), w2_words[0].bitcast(I32))
         w2_rows = w2_scales[0].rearrange("(b r) n -> r b n", r=4)
         for r in range(4):
@@ -136,7 +134,7 @@ def tile_moe_sdn_glu_relu_kernel(
                         nc.tensor.matmul_mx(
                             out=bank[:, (e - e0) * C : (e - e0 + 1) * C],
                             lhsT=words[q // 2, g, m][:, (e - e0) * PASSES + s, 2 * cols.start : 2 * cols.stop].bitcast(FP4X4),
-                            lhsT_scale=planes[min(g, 1)][m][:, (e - SCALE_LOADS[min(g, 1)][0]) * PASSES + s, P * q : P * (q + 1)],
+                            lhsT_scale=planes[q // 2][m][:, e * PASSES + s, cols],
                             rhs=gx[s][:, slots].bitcast(FP8X4),
                             rhs_scale=gs[s][:, slots],
                             start=(s == 0),

@@ -57,13 +57,12 @@ def tile_moe_sdn_glu_relu_kernel(
         words = {}
 
         nc.gpsimd.memset(xs[:].bitcast(I32), 0)
-        nc.vector.memset(planes[0][0][:].bitcast(I32), 0)
+        for pair in planes:
+            for plane in pair:
+                nc.vector.memset(plane[:].bitcast(I32), 0)
         gate_rows = keep.tile([P, P], F32, name="gate_rows")
         nc.gpsimd.memset(gate_rows[:], 0.0)
-        nc.gpsimd.memset(planes[0][1][:].bitcast(I32), 0)
         make_identity(nc, ident[:])
-        nc.gpsimd.memset(planes[1][0][:].bitcast(I32), 0)
-        nc.gpsimd.memset(planes[1][1][:].bitcast(I32), 0)
         nc.gpsimd.memset(w2s[:].bitcast(I32), 0)
 
         def load_words(half, g):

@@ -25,7 +25,7 @@ HQ = H // P
 GROUPS = ((0, 4), (4, 8), (8, 10))
 GATE_ROWS = 8
 GATE_RUN = T // GATE_ROWS
-GATHERS = ((0, 384), (384, 768), (768, 1024), (1024, 1280))
+SPARE = 64
 CHUNKS = ((0, 256), (256, 384), (384, 512), (512, 640))
 
 
@@ -40,8 +40,8 @@ def tile_moe_sdn_glu_relu_kernel(
 
         offs_t = keep.tile([P, S // 16], U16, name="offs_t")
         pos_t = [keep.tile([P, T // 16], U16, name=f"pos_t{r}") for r in range(2)]
-        xw = [keep.tile([P, T], I32, name=f"xw{s}", align_bytes=64) for s in range(PASSES)]
-        xs = keep.tile([P, PASSES, T], U8, name="xs", align_bytes=64)
+        xw = keep.tile([P, PASSES * T + SPARE], I32, name="xw", align_bytes=64)
+        xs = keep.tile([P, PASSES * T + SPARE], U8, name="xs", align_bytes=64)
         w2w = keep.tile([P, 2 * N], U8, name="w2w", align_bytes=64)
         w2s = keep.tile([P, N], U8, name="w2s", align_bytes=64)
         gate_t = keep.tile([P, 2, T], F32, name="gate_t")
@@ -56,14 +56,15 @@ def tile_moe_sdn_glu_relu_kernel(
         ]
         words = {}
 
-        nc.gpsimd.memset(xs[:].bitcast(I32), 0)
+        make_identity(nc, ident[:])
+        gate_rows = keep.tile([P, P], F32, name="gate_rows")
+        nc.vector.memset(xs[:].bitcast(I32), 0)
+        nc.vector.memset(gate_rows[:], 0.0)
         for pair in planes:
             for plane in pair:
                 nc.vector.memset(plane[:].bitcast(I32), 0)
-        gate_rows = keep.tile([P, P], F32, name="gate_rows")
-        nc.gpsimd.memset(gate_rows[:], 0.0)
-        make_identity(nc, ident[:])
-        nc.gpsimd.memset(w2s[:].bitcast(I32), 0)
+        nc.vector.memset(xw[:, PASSES * T :], 0)
+        nc.vector.memset(w2s[:].bitcast(I32), 0)
 
         def load_words(half, g):
             e0, e1 = GROUPS[g]
@@ -82,10 +83,11 @@ def tile_moe_sdn_glu_relu_kernel(
 
         nc.sync.dma_start(offs_t[:], offs)
         for s in range(PASSES):
-            nc.sync.dma_start(xw[s][:], x_words[s].rearrange("p t d -> p (t d)").bitcast(I32))
+            nc.sync.dma_start(xw[:, s * T : (s + 1) * T], x_words[s].rearrange("p t d -> p (t d)").bitcast(I32))
         xs_rows = x_scales.rearrange("s (b r) t -> r b s t", r=4)
         for r in range(4):
-            nc.sync.dma_start(xs[r:P:32, :, :].bitcast(I32), xs_rows[r].bitcast(I32))
+            rows = xs[r:P:32, : PASSES * T].rearrange("b (s t) -> b s t", s=PASSES)
+            nc.sync.dma_start(rows.bitcast(I32), xs_rows[r].bitcast(I32))
         nc.sync.dma_start(gate_rows[: 2 * GATE_ROWS, :GATE_RUN], gate[:, 0, :].rearrange("r (a t) -> r a t", t=GATE_RUN))
         load_scales(0)
         for g in range(len(GROUPS)):
@@ -115,15 +117,15 @@ def tile_moe_sdn_glu_relu_kernel(
         def gather_tokens(c0, c1):
             lst = offs_t[:, c0 // 16 : c1 // 16]
             for s in range(PASSES):
-                nc.vector.tensor_copy(gx[s][:, c0:c1], xw[s][:].bitcast(U32).indirect(lst))
+                nc.vector.tensor_copy(gx[s][:, c0:c1], xw[:, s * T : (s + 1) * T + SPARE].bitcast(U32).indirect(lst))
             for s in range(PASSES):
-                nc.vector.tensor_copy(gs[s][:, c0:c1], xs[:, s, :].indirect(lst))
+                nc.vector.tensor_copy(gs[s][:, c0:c1], xs[:, s * T : (s + 1) * T + SPARE].indirect(lst))
 
         def unit(q, g, pair):
             e0, e1 = GROUPS[g]
             width = (e1 - e0) * C
             direct = g == len(GROUPS) - 1
-            sums = keep.tile([P, 1 if direct else 2, width], F32, name=f"sums{q}_{g}", align_bytes=64)
+            sums = keep.tile([P, 1 if direct else 2, width], F32, name=f"sums{q}_{g}", tag=f"sums{q}_{g}", align_bytes=64)
             for m in range(2):
                 bank = banks[pair[m]]
                 cols = slice(P * (q % 2), P * (q % 2 + 1))
@@ -210,8 +212,8 @@ def tile_moe_sdn_glu_relu_kernel(
             copy(res[:], bank[:, : 2 * n].rearrange("p (a t) -> p a t", a=2))
             nc.sync.dma_start(out_v[:, :, t0:t1], res[:])
 
-        for c0, c1 in GATHERS:
-            gather_tokens(c0, c1)
+        for e0, e1 in GROUPS:
+            gather_tokens(e0 * C, e1 * C)
         unit(0, 0, (0, 1))
         unit(1, 0, (2, 3))
         unit(0, 1, (4, 5))
@@ -225,7 +227,7 @@ def tile_moe_sdn_glu_relu_kernel(
         unit(2, 1, (0, 1))
         unit(3, 1, (2, 3))
         unit(2, 2, (4, 5))
-        y2 = [pick(2, *CHUNKS[0])]
+        y2 = pick(2, 0, CHUNKS[1][1])
         unit(3, 2, (6, 7))
         by_scalar, by_vector = nc.scalar.copy, nc.vector.tensor_copy
         early = ((banks[4], (0,)), (banks[6], (1, 2)), (banks[4], (3,)))
@@ -239,12 +241,14 @@ def tile_moe_sdn_glu_relu_kernel(
             for copy in copies:
                 copy()
         last = len(CHUNKS) - 1
+        first = 0
         for c, (t0, t1) in enumerate(CHUNKS):
-            if c > 0:
-                y2.append(pick(2, t0, t1))
+            if c == 2:
+                late = keep.tile([P, 2, T - t0], F32, name="late", tag="sums3_2", align_bytes=64)
+                y2, first = pick(2, t0, T, late[:]), t0
             y3 = pick(3, t0, t1)
             ring = (0, 1, 2) if c % 2 == 0 else (3, 5, 7)
             edge = by_vector if c == last else by_scalar
-            turn(1, c, (y2[c], y3), banks[ring[0]][:, : 2 * (t1 - t0)], edge)()
+            turn(1, c, (y2[:, :, t0 - first : t1 - first], y3), banks[ring[0]][:, : 2 * (t1 - t0)], edge)()
             grouped = turn_back(c, banks[ring[1]], by_scalar)
             project(t0, t1, grouped, banks[ring[2]], edge)

@@ -26,6 +26,7 @@ GROUPS = ((0, 4), (4, 8), (8, 10))
 GATE_ROWS = 8
 GATE_RUN = T // GATE_ROWS
 SPARE = 64
+SPLIT = 6
 CHUNKS = ((0, 256), (256, 384), (384, 512), (512, 640))
 
 
@@ -56,9 +57,9 @@ def tile_moe_sdn_glu_relu_kernel(
         ]
         words = {}
 
+        nc.gpsimd.memset(xs[:].bitcast(I32), 0)
         make_identity(nc, ident[:])
         gate_rows = keep.tile([P, P], F32, name="gate_rows")
-        nc.vector.memset(xs[:].bitcast(I32), 0)
         nc.vector.memset(gate_rows[:], 0.0)
         for pair in planes:
             for plane in pair:
@@ -66,13 +67,13 @@ def tile_moe_sdn_glu_relu_kernel(
         nc.vector.memset(xw[:, PASSES * T :], 0)
         nc.vector.memset(w2s[:].bitcast(I32), 0)
 
-        def load_words(half, g):
-            e0, e1 = GROUPS[g]
-            for m, src in enumerate((w1_words, w3_words)):
-                rows = src[e0:e1].rearrange("e s p b -> p (e s) b")[:, :, 4 * P * half : 4 * P * (half + 1)]
-                tile = keep.tile([P, (e1 - e0) * PASSES, 4 * P], U8, name=f"words{half}_{g}_{m}", align_bytes=64)
-                words[half, g, m] = tile
-                nc.sync.dma_start(tile[:].bitcast(I32), rows.bitcast(I32))
+        def load_words(m, e0, e1, q0, q1):
+            rows = (w1_words, w3_words)[m][e0:e1].rearrange("e s p b -> p (e s) b")[:, :, 2 * P * q0 : 2 * P * q1]
+            tile = keep.tile([P, (e1 - e0) * PASSES, 2 * P * (q1 - q0)], U8, name=f"words{m}_{e0}_{q0}", align_bytes=64)
+            nc.sync.dma_start(tile[:].bitcast(I32), rows.bitcast(I32))
+            for e in range(e0, e1):
+                for q in range(q0, q1):
+                    words[m, e, q] = tile[:, (e - e0) * PASSES : (e - e0 + 1) * PASSES, 2 * P * (q - q0) : 2 * P * (q - q0 + 1)]
 
         def load_scales(half):
             for plane, src in zip(planes[half], (w1_scales, w3_scales)):
@@ -82,16 +83,23 @@ def tile_moe_sdn_glu_relu_kernel(
                     nc.sync.dma_start(plane[r:P:32, :, :].bitcast(I32), part.bitcast(I32))
 
         nc.sync.dma_start(offs_t[:], offs)
-        for s in range(PASSES):
-            nc.sync.dma_start(xw[:, s * T : (s + 1) * T], x_words[s].rearrange("p t d -> p (t d)").bitcast(I32))
         xs_rows = x_scales.rearrange("s (b r) t -> r b s t", r=4)
         for r in range(4):
             rows = xs[r:P:32, : PASSES * T].rearrange("b (s t) -> b s t", s=PASSES)
-            nc.sync.dma_start(rows.bitcast(I32), xs_rows[r].bitcast(I32))
+            nc.scalar.dma_start(rows.bitcast(I32), xs_rows[r].bitcast(I32))
+        nc.sync.dma_start(
+            xw[:, : PASSES * T].rearrange("p (s t) -> p s t", s=PASSES),
+            x_words.rearrange("s p t d -> p s (t d)").bitcast(I32),
+        )
         nc.sync.dma_start(gate_rows[: 2 * GATE_ROWS, :GATE_RUN], gate[:, 0, :].rearrange("r (a t) -> r a t", t=GATE_RUN))
+        load_words(0, *GROUPS[0], 0, 2)
         load_scales(0)
-        for g in range(len(GROUPS)):
-            load_words(0, g)
+        load_words(1, *GROUPS[0], 0, 2)
+        for m in range(2):
+            load_words(m, GROUPS[1][0], SPLIT, 0, 2)
+            load_words(m, SPLIT, GROUPS[1][1], 0, 3)
+        for m in range(2):
+            load_words(m, *GROUPS[2], 0, 3)
         for r, pos in enumerate((pos1, pos2)):
             nc.sync.dma_start(pos_t[r][:], pos)
         load_scales(1)
@@ -107,8 +115,9 @@ def tile_moe_sdn_glu_relu_kernel(
                 nc.tensor.transpose(bank[:, j * P : (j + 1) * P], column.to_broadcast([P, P]), ident[:])
             nc.scalar.copy(gate_runs[:, c0 : c0 + 4, :], bank[:].rearrange("p (j t) -> p j t", t=P)[:, :, :GATE_RUN])
 
-        for g in range(len(GROUPS)):
-            load_words(1, g)
+        for e0, e1, q0, q1 in ((*GROUPS[0], 2, 4), (GROUPS[1][0], SPLIT, 2, 4), (SPLIT, GROUPS[1][1], 3, 4), (*GROUPS[2], 3, 4)):
+            for m in range(2):
+                load_words(m, e0, e1, q0, q1)
         nc.sync.dma_start(w2w[:].bitcast(I32), w2_words[0].bitcast(I32))
         w2_rows = w2_scales[0].rearrange("(b r) n -> r b n", r=4)
         for r in range(4):
@@ -121,20 +130,19 @@ def tile_moe_sdn_glu_relu_kernel(
             for s in range(PASSES):
                 nc.vector.tensor_copy(gs[s][:, c0:c1], xs[:, s * T : (s + 1) * T + SPARE].indirect(lst))
 
-        def unit(q, g, pair):
+        def unit(q, g, pair, direct=False):
             e0, e1 = GROUPS[g]
             width = (e1 - e0) * C
-            direct = g == len(GROUPS) - 1
             sums = keep.tile([P, 1 if direct else 2, width], F32, name=f"sums{q}_{g}", tag=f"sums{q}_{g}", align_bytes=64)
             for m in range(2):
                 bank = banks[pair[m]]
                 cols = slice(P * (q % 2), P * (q % 2 + 1))
-                for e in range(e0, e1):
+                for e in sorted(range(e0, e1), key=lambda e: q == 2 and e < SPLIT):
                     slots = slice(e * C, (e + 1) * C)
                     for s in range(PASSES):
                         nc.tensor.matmul_mx(
                             out=bank[:, (e - e0) * C : (e - e0 + 1) * C],
-                            lhsT=words[q // 2, g, m][:, (e - e0) * PASSES + s, 2 * cols.start : 2 * cols.stop].bitcast(FP4X4),
+                            lhsT=words[m, e, q][:, s, :].bitcast(FP4X4),
                             lhsT_scale=planes[q // 2][m][:, e * PASSES + s, cols],
                             rhs=gx[s][:, slots].bitcast(FP8X4),
                             rhs_scale=gs[s][:, slots],
@@ -158,13 +166,14 @@ def tile_moe_sdn_glu_relu_kernel(
                 )
             return y
 
-        def turn(half, c, ys, into, copy):
+        def turn(q0, c, ys, into, copy):
             tiles = (CHUNKS[c][1] - CHUNKS[c][0]) // P
-            for qq in range(2):
+            nq = len(ys)
+            for qq in range(nq):
                 for j in range(tiles):
                     for r in range(2):
                         nc.tensor.matmul(
-                            into[:, (2 * j + qq) * P : (2 * j + qq + 1) * P],
+                            into[:, (nq * j + qq) * P : (nq * j + qq + 1) * P],
                             lhsT=ys[qq][:, r, j * P : (j + 1) * P],
                             rhs=ident[:],
                             start=(r == 0),
@@ -172,8 +181,8 @@ def tile_moe_sdn_glu_relu_kernel(
                             is_transpose=True,
                         )
             return lambda: copy(
-                ct[c][:, :, :, 64 * half : 64 * (half + 1), :],
-                into.rearrange("t (j p u e) -> t j u p e", p=64, u=2, e=2),
+                ct[c][:, :, :, 32 * q0 : 32 * (q0 + nq), :],
+                into.rearrange("t (j p u e) -> t j u p e", p=32 * nq, u=2, e=2),
             )
 
         out_v = out.rearrange("(a p) t -> p a t", p=P)
@@ -218,19 +227,19 @@ def tile_moe_sdn_glu_relu_kernel(
         unit(1, 0, (2, 3))
         unit(0, 1, (4, 5))
         unit(1, 1, (6, 7))
-        unit(0, 2, (0, 1))
+        unit(0, 2, (0, 1), direct=True)
         y0 = pick(0, 0, T)
-        unit(1, 2, (2, 3))
+        unit(1, 2, (2, 3), direct=True)
         y1 = pick(1, 0, T)
-        unit(2, 0, (4, 5))
-        unit(3, 0, (6, 7))
-        unit(2, 1, (0, 1))
-        unit(3, 1, (2, 3))
         unit(2, 2, (4, 5))
+        unit(2, 0, (6, 7))
+        unit(3, 0, (0, 1))
+        unit(2, 1, (2, 3), direct=True)
         y2 = pick(2, 0, CHUNKS[1][1])
-        unit(3, 2, (6, 7))
+        unit(3, 1, (4, 5))
+        unit(3, 2, (6, 7), direct=True)
         by_scalar, by_vector = nc.scalar.copy, nc.vector.tensor_copy
-        early = ((banks[4], (0,)), (banks[6], (1, 2)), (banks[4], (3,)))
+        early = ((banks[2], (0,)), (banks[6], (1, 2)), (banks[2], (3,)))
         for bank, chunks in early:
             copies = []
             for place, c in enumerate(chunks):
@@ -249,6 +258,11 @@ def tile_moe_sdn_glu_relu_kernel(
             y3 = pick(3, t0, t1)
             ring = (0, 1, 2) if c % 2 == 0 else (3, 5, 7)
             edge = by_vector if c == last else by_scalar
-            turn(1, c, (y2[:, :, t0 - first : t1 - first], y3), banks[ring[0]][:, : 2 * (t1 - t0)], edge)()
-            grouped = turn_back(c, banks[ring[1]], by_scalar)
+            ys = (y2[:, :, t0 - first : t1 - first], y3)
+            if c == last:
+                turn(2, c, ys[:1], banks[6][:, : t1 - t0], by_scalar)()
+                turn(3, c, ys[1:], banks[ring[0]][:, : t1 - t0], by_vector)()
+            else:
+                turn(2, c, ys, banks[ring[0]][:, : 2 * (t1 - t0)], by_scalar)()
+            grouped = turn_back(c, banks[ring[1]], by_vector if c == last - 1 else by_scalar)
             project(t0, t1, grouped, banks[ring[2]], edge)

@@ -41,18 +41,18 @@ def tile_moe_sdn_glu_relu_kernel(
 
         offs_t = keep.tile([P, S // 16], U16, name="offs_t")
         pos_t = [keep.tile([P, T // 16], U16, name=f"pos_t{r}") for r in range(2)]
-        xw = keep.tile([P, PASSES * T + SPARE], I32, name="xw", align_bytes=64)
-        xs = keep.tile([P, PASSES * T + SPARE], U8, name="xs", align_bytes=64)
-        w2w = keep.tile([P, 2 * N], U8, name="w2w", align_bytes=64)
-        w2s = keep.tile([P, N], U8, name="w2s", align_bytes=64)
+        xw = keep.tile([P, PASSES * T + SPARE], I32, name="xw", align_bytes=256)
+        xs = keep.tile([P, PASSES * T + SPARE], U8, name="xs", align_bytes=256)
+        w2w = keep.tile([P, 2 * N], U8, name="w2w", align_bytes=256)
+        w2s = keep.tile([P, N], U8, name="w2s", align_bytes=256)
         gate_t = keep.tile([P, 2, T], F32, name="gate_t")
         ident = keep.tile([P, P], F32, name="ident")
-        gx = [keep.tile([P, S], U32, name=f"gx{s}", align_bytes=64) for s in range(PASSES)]
-        gs = [keep.tile([P, S], U8, name=f"gs{s}", align_bytes=64) for s in range(PASSES)]
+        gx = [keep.tile([P, S], U32, name=f"gx{s}", align_bytes=256) for s in range(PASSES)]
+        gs = [keep.tile([P, S], U8, name=f"gs{s}", align_bytes=256) for s in range(PASSES)]
         h = [keep.tile([P, S], F32, name=f"h{q}") for q in range(HQ)]
-        ct = [keep.tile([P, (t1 - t0) // P, 2, P, 2], BF16, name=f"ct{t0}", align_bytes=64) for t0, t1 in CHUNKS]
+        ct = [keep.tile([P, (t1 - t0) // P, 2, P, 2], BF16, name=f"ct{t0}", align_bytes=256) for t0, t1 in CHUNKS]
         planes = [
-            [keep.tile([P, E * PASSES, 2 * P], U8, name=f"plane{half}_{m}", align_bytes=64) for m in range(2)]
+            [keep.tile([P, E * PASSES, 2 * P], U8, name=f"plane{half}_{m}", align_bytes=256) for m in range(2)]
             for half in range(2)
         ]
         words = {}
@@ -69,7 +69,7 @@ def tile_moe_sdn_glu_relu_kernel(
 
         def load_words(m, e0, e1, q0, q1):
             rows = (w1_words, w3_words)[m][e0:e1].rearrange("e s p b -> p (e s) b")[:, :, 2 * P * q0 : 2 * P * q1]
-            tile = keep.tile([P, (e1 - e0) * PASSES, 2 * P * (q1 - q0)], U8, name=f"words{m}_{e0}_{q0}", align_bytes=64)
+            tile = keep.tile([P, (e1 - e0) * PASSES, 2 * P * (q1 - q0)], U8, name=f"words{m}_{e0}_{q0}", align_bytes=256)
             nc.sync.dma_start(tile[:].bitcast(I32), rows.bitcast(I32))
             for e in range(e0, e1):
                 for q in range(q0, q1):
@@ -133,7 +133,7 @@ def tile_moe_sdn_glu_relu_kernel(
         def unit(q, g, pair, direct=False):
             e0, e1 = GROUPS[g]
             width = (e1 - e0) * C
-            sums = keep.tile([P, 1 if direct else 2, width], F32, name=f"sums{q}_{g}", tag=f"sums{q}_{g}", align_bytes=64)
+            sums = keep.tile([P, 1 if direct else 2, width], F32, name=f"sums{q}_{g}", tag=f"sums{q}_{g}", align_bytes=256)
             for m in range(2):
                 bank = banks[pair[m]]
                 cols = slice(P * (q % 2), P * (q % 2 + 1))
@@ -190,7 +190,7 @@ def tile_moe_sdn_glu_relu_kernel(
         def turn_back(c, bank, copy):
             t0, t1 = CHUNKS[c]
             n = t1 - t0
-            grouped = keep.tile([P, n, 4], BF16, name=f"grouped{t0}", align_bytes=64)
+            grouped = keep.tile([P, n, 4], BF16, name=f"grouped{t0}", align_bytes=256)
             pairs = ct[c][:].rearrange("t j u p e -> t (j u p e)").bitcast(F32)
             for b in range(2 * n // P):
                 nc.tensor.transpose(bank[:, b * P : (b + 1) * P], pairs[:, b * P : (b + 1) * P], ident[:])
@@ -202,8 +202,8 @@ def tile_moe_sdn_glu_relu_kernel(
 
         def project(t0, t1, grouped, bank, copy):
             n = t1 - t0
-            codes = keep.tile([P, n], U32, name=f"codes{t0}", align_bytes=64)
-            cs = keep.tile([P, n], U8, name=f"cs{t0}", align_bytes=64)
+            codes = keep.tile([P, n], U32, name=f"codes{t0}", align_bytes=256)
+            cs = keep.tile([P, n], U8, name=f"cs{t0}", align_bytes=256)
             nc.vector.quantize_mx(
                 out=codes[:].bitcast(FP8X4), scales=cs[:], in_=grouped[:].rearrange("p t j -> p (t j)")
             )
@@ -217,7 +217,7 @@ def tile_moe_sdn_glu_relu_kernel(
                     start=True,
                     stop=True,
                 )
-            res = keep.tile([P, 2, n], F32, name=f"res{t0}")
+            res = keep.tile([P, 2, n], F32, name=f"res{t0}", align_bytes=256)
             copy(res[:], bank[:, : 2 * n].rearrange("p (a t) -> p a t", a=2))
             nc.sync.dma_start(out_v[:, :, t0:t1], res[:])
 
@@ -253,7 +253,7 @@ def tile_moe_sdn_glu_relu_kernel(
         first = 0
         for c, (t0, t1) in enumerate(CHUNKS):
             if c == 2:
-                late = keep.tile([P, 2, T - t0], F32, name="late", tag="sums3_2", align_bytes=64)
+                late = keep.tile([P, 2, T - t0], F32, name="late", tag="sums3_2", align_bytes=256)
                 y2, first = pick(2, t0, T, late[:]), t0
             y3 = pick(3, t0, t1)
             ring = (0, 1, 2) if c % 2 == 0 else (3, 5, 7)

@@ -15,19 +15,19 @@ U8 = mybir.dt.uint8
 FP8X4 = mybir.dt.float8_e4m3fn_x4
 FP4X4 = mybir.dt.float4_e2m1fn_x4
 MULT = mybir.AluOpType.mult
+ADD = mybir.AluOpType.add
 RELU = mybir.ActivationFunctionType.Relu
+COPY = mybir.ActivationFunctionType.Copy
 
 P = 128
 BANK = 512
 S = E * C
 PASSES = K // 512
 HQ = H // P
+TILES = T // P
 GROUPS = ((0, 4), (4, 8), (8, 10))
-GATE_ROWS = 8
-GATE_RUN = T // GATE_ROWS
+GATED = 3
 SPARE = 64
-SPLIT = 6
-CHUNKS = ((0, 256), (256, 384), (384, 512), (512, 640))
 
 
 def tile_moe_sdn_glu_relu_kernel(
@@ -45,12 +45,13 @@ def tile_moe_sdn_glu_relu_kernel(
         xs = keep.tile([P, PASSES * T + SPARE], U8, name="xs", align_bytes=256)
         w2w = keep.tile([P, 2 * N], U8, name="w2w", align_bytes=256)
         w2s = keep.tile([P, N], U8, name="w2s", align_bytes=256)
-        gate_t = keep.tile([P, 2, T], F32, name="gate_t")
+        gate_t = keep.tile([P, 2, GATED * P], F32, name="gate_t")
+        gate_cols = keep.tile([P, 2 * TILES], F32, name="gate_cols")
         ident = keep.tile([P, P], F32, name="ident")
         gx = [keep.tile([P, S], U32, name=f"gx{s}", align_bytes=256) for s in range(PASSES)]
         gs = [keep.tile([P, S], U8, name=f"gs{s}", align_bytes=256) for s in range(PASSES)]
         h = [keep.tile([P, S], F32, name=f"h{q}") for q in range(HQ)]
-        ct = [keep.tile([P, (t1 - t0) // P, 2, P, 2], BF16, name=f"ct{t0}", align_bytes=256) for t0, t1 in CHUNKS]
+        ct = [keep.tile([P, H], BF16, name=f"ct{j}", align_bytes=256) for j in range(TILES)]
         planes = [
             [keep.tile([P, E * PASSES, 2 * P], U8, name=f"plane{half}_{m}", align_bytes=256) for m in range(2)]
             for half in range(2)
@@ -58,9 +59,9 @@ def tile_moe_sdn_glu_relu_kernel(
         words = {}
 
         nc.gpsimd.memset(xs[:].bitcast(I32), 0)
-        make_identity(nc, ident[:])
         gate_rows = keep.tile([P, P], F32, name="gate_rows")
-        nc.vector.memset(gate_rows[:], 0.0)
+        nc.gpsimd.memset(gate_rows[:], 0.0)
+        make_identity(nc, ident[:])
         for pair in planes:
             for plane in pair:
                 nc.vector.memset(plane[:].bitcast(I32), 0)
@@ -75,49 +76,46 @@ def tile_moe_sdn_glu_relu_kernel(
                 for q in range(q0, q1):
                     words[m, e, q] = tile[:, (e - e0) * PASSES : (e - e0 + 1) * PASSES, 2 * P * (q - q0) : 2 * P * (q - q0 + 1)]
 
-        def load_scales(half):
-            for plane, src in zip(planes[half], (w1_scales, w3_scales)):
-                rows = src.rearrange("e s (b r) i -> r b (e s) i", r=4)
-                for r in range(4):
-                    part = rows[r][:, :, 2 * P * half : 2 * P * (half + 1)]
-                    nc.sync.dma_start(plane[r:P:32, :, :].bitcast(I32), part.bitcast(I32))
+        def load_scales(m, half, e0, e1):
+            rows = (w1_scales, w3_scales)[m].rearrange("e s (b r) i -> r b (e s) i", r=4)
+            for r in range(4):
+                part = rows[r][:, e0 * PASSES : e1 * PASSES, 2 * P * half : 2 * P * (half + 1)]
+                nc.sync.dma_start(planes[half][m][r:P:32, e0 * PASSES : e1 * PASSES, :].bitcast(I32), part.bitcast(I32))
 
+        nc.sync.dma_start(
+            xw[:, : PASSES * T].rearrange("p (s t) -> p s t", s=PASSES),
+            x_words.rearrange("s p t d -> p s (t d)").bitcast(I32),
+        )
         nc.sync.dma_start(offs_t[:], offs)
         xs_rows = x_scales.rearrange("s (b r) t -> r b s t", r=4)
         for r in range(4):
             rows = xs[r:P:32, : PASSES * T].rearrange("b (s t) -> b s t", s=PASSES)
             nc.scalar.dma_start(rows.bitcast(I32), xs_rows[r].bitcast(I32))
-        nc.sync.dma_start(
-            xw[:, : PASSES * T].rearrange("p (s t) -> p s t", s=PASSES),
-            x_words.rearrange("s p t d -> p s (t d)").bitcast(I32),
-        )
-        nc.sync.dma_start(gate_rows[: 2 * GATE_ROWS, :GATE_RUN], gate[:, 0, :].rearrange("r (a t) -> r a t", t=GATE_RUN))
+        nc.sync.dma_start(gate_rows[: 2 * TILES, :], gate[:, 0, :].rearrange("r (j t) -> r j t", t=P))
         load_words(0, *GROUPS[0], 0, 2)
-        load_scales(0)
+        for m in range(2):
+            load_scales(m, 0, 0, E)
         load_words(1, *GROUPS[0], 0, 2)
-        for m in range(2):
-            load_words(m, GROUPS[1][0], SPLIT, 0, 2)
-            load_words(m, SPLIT, GROUPS[1][1], 0, 3)
-        for m in range(2):
-            load_words(m, *GROUPS[2], 0, 3)
+        for e in range(GROUPS[1][0], E, 2):
+            for m in range(2):
+                load_words(m, e, e + 2, 0, 3)
         for r, pos in enumerate((pos1, pos2)):
             nc.sync.dma_start(pos_t[r][:], pos)
-        load_scales(1)
 
         nc.tensor.transpose(banks[0][:, :P], gate_rows[:], ident[:])
-        gate_runs = gate_t[:].rearrange("p r (a t) -> p (r a) t", t=GATE_RUN)
-        for c0 in range(0, 2 * GATE_ROWS, 4):
-            gate_cols = keep.tile([P, 4], F32, name=f"gate_cols{c0}")
-            nc.scalar.copy(gate_cols[:], banks[0][:, c0 : c0 + 4])
-            bank = banks[4 + c0 // 4]
-            for j in range(4):
-                column = gate_cols[:, j : j + 1]
+        nc.scalar.copy(gate_cols[:], banks[0][:, : 2 * TILES])
+        for r in range(2):
+            bank = banks[4 + r]
+            for j in range(GATED):
+                column = gate_cols[:, r * TILES + j : r * TILES + j + 1]
                 nc.tensor.transpose(bank[:, j * P : (j + 1) * P], column.to_broadcast([P, P]), ident[:])
-            nc.scalar.copy(gate_runs[:, c0 : c0 + 4, :], bank[:].rearrange("p (j t) -> p j t", t=P)[:, :, :GATE_RUN])
-
-        for e0, e1, q0, q1 in ((*GROUPS[0], 2, 4), (GROUPS[1][0], SPLIT, 2, 4), (SPLIT, GROUPS[1][1], 3, 4), (*GROUPS[2], 3, 4)):
+            nc.scalar.copy(gate_t[:, r, :], bank[:, : GATED * P])
+        for m in range(2):
+            load_scales(m, 1, 0, E)
+            load_words(m, *GROUPS[0], 2, 4)
+        for e in range(GROUPS[1][0], E, 2):
             for m in range(2):
-                load_words(m, e0, e1, q0, q1)
+                load_words(m, e, e + 2, 3, 4)
         nc.sync.dma_start(w2w[:].bitcast(I32), w2_words[0].bitcast(I32))
         w2_rows = w2_scales[0].rearrange("(b r) n -> r b n", r=4)
         for r in range(4):
@@ -130,83 +128,115 @@ def tile_moe_sdn_glu_relu_kernel(
             for s in range(PASSES):
                 nc.vector.tensor_copy(gs[s][:, c0:c1], xs[:, s * T : (s + 1) * T + SPARE].indirect(lst))
 
-        def unit(q, g, pair, direct=False):
-            e0, e1 = GROUPS[g]
-            width = (e1 - e0) * C
-            sums = keep.tile([P, 1 if direct else 2, width], F32, name=f"sums{q}_{g}", tag=f"sums{q}_{g}", align_bytes=256)
+        def product(m, q, experts, into):
+            e0, e1 = experts
+            for e in range(e0, e1):
+                slots = slice(e * C, (e + 1) * C)
+                for s in range(PASSES):
+                    nc.tensor.matmul_mx(
+                        out=into[:, (e - e0) * C : (e - e0 + 1) * C],
+                        lhsT=words[m, e, q][:, s, :].bitcast(FP4X4),
+                        lhsT_scale=planes[q // 2][m][:, e * PASSES + s, P * (q % 2) : P * (q % 2 + 1)],
+                        rhs=gx[s][:, slots].bitcast(FP8X4),
+                        rhs_scale=gs[s][:, slots],
+                        start=(s == 0),
+                        stop=(s == PASSES - 1),
+                    )
+
+        active = {}
+
+        def activate(q, experts, sums):
+            e0, e1 = experts
+            active[q, e0] = keep.tile([P, (e1 - e0) * C], F32, name=f"active{q}_{e0}", align_bytes=256)
+            nc.scalar.activation(active[q, e0][:], sums, RELU)
+
+        def multiply(q, experts, sums, parked):
+            e0, e1 = experts
+            if parked:
+                kept = keep.tile([P, (e1 - e0) * C], F32, name=f"parked{q}_{e0}", align_bytes=256)
+                nc.scalar.copy(kept[:], sums)
+                sums = kept[:]
+            nc.vector.tensor_tensor(h[q][:, e0 * C : e1 * C], sums, active[q, e0][:], MULT)
+
+        def first(q, experts, bank):
+            sums = bank[:, : (experts[1] - experts[0]) * C]
+            product(0, q, experts, sums)
+            activate(q, experts, sums)
+
+        def second(q, experts, bank, parked=False):
+            sums = bank[:, : (experts[1] - experts[0]) * C]
+            product(1, q, experts, sums)
+            multiply(q, experts, sums, parked)
+
+        def both(q, experts, bank, parked=False):
             for m in range(2):
-                bank = banks[pair[m]]
-                cols = slice(P * (q % 2), P * (q % 2 + 1))
-                for e in sorted(range(e0, e1), key=lambda e: q == 2 and e < SPLIT):
-                    slots = slice(e * C, (e + 1) * C)
-                    for s in range(PASSES):
-                        nc.tensor.matmul_mx(
-                            out=bank[:, (e - e0) * C : (e - e0 + 1) * C],
-                            lhsT=words[m, e, q][:, s, :].bitcast(FP4X4),
-                            lhsT_scale=planes[q // 2][m][:, e * PASSES + s, cols],
-                            rhs=gx[s][:, slots].bitcast(FP8X4),
-                            rhs_scale=gs[s][:, slots],
-                            start=(s == 0),
-                            stop=(s == PASSES - 1),
-                        )
-                if m == 0:
-                    nc.scalar.activation(sums[:, 0, :], bank[:, :width], RELU)
-                elif not direct:
-                    nc.scalar.copy(sums[:, 1, :], bank[:, :width])
-            other = banks[pair[1]][:, :width] if direct else sums[:, 1, :]
-            nc.vector.tensor_tensor(h[q][:, e0 * C : e1 * C], other, sums[:, 0, :], MULT)
-            return sums
+                product(m, q, experts, bank[:, 2 * C * m : 2 * C * (m + 1)])
+            activate(q, experts, bank[:, : 2 * C])
+            multiply(q, experts, bank[:, 2 * C :], parked)
 
-        def pick(q, t0, t1, y=None):
-            if y is None:
-                y = keep.tile([P, 2, t1 - t0], F32, name=f"y{q}_{t0}")[:]
+        picked = {}
+
+        def pick(q, j0, j1, gated):
+            t0, t1 = j0 * P, j1 * P
+            y = keep.tile([P, 2, t1 - t0], F32, name=f"y{q}_{j0}", align_bytes=256)
             for r in range(2):
-                nc.vector.tensor_tensor(
-                    y[:, r, :], h[q][:].indirect(pos_t[r][:, t0 // 16 : t1 // 16]), gate_t[:, r, t0:t1], MULT
-                )
-            return y
+                found = h[q][:].indirect(pos_t[r][:, t0 // 16 : t1 // 16])
+                if gated:
+                    nc.vector.tensor_tensor(y[:, r, :], found, gate_t[:, r, t0:t1], MULT)
+                else:
+                    nc.scalar.activation(y[:, r, :], found, COPY)
+            for j in range(j0, j1):
+                picked[q, j] = y[:, :, (j - j0) * P : (j - j0 + 1) * P]
 
-        def turn(q0, c, ys, into, copy):
-            tiles = (CHUNKS[c][1] - CHUNKS[c][0]) // P
-            nq = len(ys)
-            for qq in range(nq):
-                for j in range(tiles):
-                    for r in range(2):
-                        nc.tensor.matmul(
-                            into[:, (nq * j + qq) * P : (nq * j + qq + 1) * P],
-                            lhsT=ys[qq][:, r, j * P : (j + 1) * P],
-                            rhs=ident[:],
-                            start=(r == 0),
-                            stop=(r == 1),
-                            is_transpose=True,
-                        )
+        def turn_gated(q0, q1, j, into, copy):
+            for q in range(q0, q1):
+                for r in range(2):
+                    nc.tensor.matmul(
+                        into[:, (q - q0) * P : (q - q0 + 1) * P],
+                        lhsT=picked[q, j][:, r, :],
+                        rhs=ident[:],
+                        start=(r == 0),
+                        stop=(r == 1),
+                        is_transpose=True,
+                    )
             return lambda: copy(
-                ct[c][:, :, :, 32 * q0 : 32 * (q0 + nq), :],
-                into.rearrange("t (j p u e) -> t j u p e", p=32 * nq, u=2, e=2),
+                ct[j][:].rearrange("t (u p e) -> t u p e", u=2, e=2)[:, :, 32 * q0 : 32 * q1, :],
+                into.rearrange("t (p u e) -> t u p e", u=2, e=2),
             )
+
+        def turn_plain(q0, q1, j, into_first, into_second):
+            width = (q1 - q0) * P
+            for q in range(q0, q1):
+                for r, into in enumerate((into_first, into_second)):
+                    nc.tensor.transpose(into[:, (q - q0) * P : (q - q0 + 1) * P], picked[q, j][:, r, :], ident[:])
+
+            def combine():
+                first = keep.tile([P, width], F32, name=f"first{q0}_{j}", align_bytes=256)
+                nc.scalar.activation(first[:], into_first, COPY, scale=gate_cols[:, j : j + 1])
+                nc.vector.scalar_tensor_tensor(
+                    ct[j][:, q0 * P : q1 * P], into_second, gate_cols[:, TILES + j : TILES + j + 1], first[:], MULT, ADD
+                )
+
+            return combine
 
         out_v = out.rearrange("(a p) t -> p a t", p=P)
 
-        def turn_back(c, bank, copy):
-            t0, t1 = CHUNKS[c]
-            n = t1 - t0
-            grouped = keep.tile([P, n, 4], BF16, name=f"grouped{t0}", align_bytes=256)
-            pairs = ct[c][:].rearrange("t j u p e -> t (j u p e)").bitcast(F32)
-            for b in range(2 * n // P):
-                nc.tensor.transpose(bank[:, b * P : (b + 1) * P], pairs[:, b * P : (b + 1) * P], ident[:])
-            copy(
+        def finish(j0, j1, back, bank, copy_back, copy_out):
+            n = (j1 - j0) * P
+            grouped = keep.tile([P, n, 4], BF16, name=f"grouped{j0}", align_bytes=256)
+            for j in range(j0, j1):
+                pairs = ct[j][:].bitcast(F32)
+                for u in range(2):
+                    b = 2 * (j - j0) + u
+                    half = pairs[:, u * P : (u + 1) * P] if j < GATED else pairs[:, u : 2 * P : 2]
+                    nc.tensor.transpose(back[:, b * P : (b + 1) * P], half, ident[:])
+            copy_back(
                 grouped[:].bitcast(F32).rearrange("p (j t) u -> p j t u", t=P),
-                bank[:, : 2 * n].rearrange("p (j u t) -> p j t u", u=2, t=P),
+                back[:, : 2 * n].rearrange("p (j u t) -> p j t u", u=2, t=P),
             )
-            return grouped
-
-        def project(t0, t1, grouped, bank, copy):
-            n = t1 - t0
-            codes = keep.tile([P, n], U32, name=f"codes{t0}", align_bytes=256)
-            cs = keep.tile([P, n], U8, name=f"cs{t0}", align_bytes=256)
-            nc.vector.quantize_mx(
-                out=codes[:].bitcast(FP8X4), scales=cs[:], in_=grouped[:].rearrange("p t j -> p (t j)")
-            )
+            codes = keep.tile([P, n], U32, name=f"codes{j0}", align_bytes=256)
+            cs = keep.tile([P, n], U8, name=f"cs{j0}", align_bytes=256)
+            nc.vector.quantize_mx(out=codes[:].bitcast(FP8X4), scales=cs[:], in_=grouped[:].rearrange("p t j -> p (t j)"))
             for a in range(2):
                 nc.tensor.matmul_mx(
                     out=bank[:, a * n : (a + 1) * n],
@@ -217,52 +247,48 @@ def tile_moe_sdn_glu_relu_kernel(
                     start=True,
                     stop=True,
                 )
-            res = keep.tile([P, 2, n], F32, name=f"res{t0}", align_bytes=256)
-            copy(res[:], bank[:, : 2 * n].rearrange("p (a t) -> p a t", a=2))
-            nc.sync.dma_start(out_v[:, :, t0:t1], res[:])
+            res = keep.tile([P, 2, n], F32, name=f"res{j0}", align_bytes=256)
+            copy_out(res[:], bank[:, : 2 * n].rearrange("p (a t) -> p a t", a=2))
+            nc.sync.dma_start(out_v[:, :, j0 * P : j1 * P], res[:])
 
+        by_scalar, by_vector = nc.scalar.copy, nc.vector.tensor_copy
         for e0, e1 in GROUPS:
             gather_tokens(e0 * C, e1 * C)
-        unit(0, 0, (0, 1))
-        unit(1, 0, (2, 3))
-        unit(0, 1, (4, 5))
-        unit(1, 1, (6, 7))
-        unit(0, 2, (0, 1), direct=True)
-        y0 = pick(0, 0, T)
-        unit(1, 2, (2, 3), direct=True)
-        y1 = pick(1, 0, T)
-        unit(2, 2, (4, 5))
-        unit(2, 0, (6, 7))
-        unit(3, 0, (0, 1))
-        unit(2, 1, (2, 3), direct=True)
-        y2 = pick(2, 0, CHUNKS[1][1])
-        unit(3, 1, (4, 5))
-        unit(3, 2, (6, 7), direct=True)
-        by_scalar, by_vector = nc.scalar.copy, nc.vector.tensor_copy
-        early = ((banks[2], (0,)), (banks[6], (1, 2)), (banks[2], (3,)))
-        for bank, chunks in early:
-            copies = []
-            for place, c in enumerate(chunks):
-                t0, t1 = CHUNKS[c]
-                width = 2 * (t1 - t0)
-                ys = [y[:, :, t0:t1] for y in (y0, y1)]
-                copies.append(turn(0, c, ys, bank[:, place * width : (place + 1) * width], by_scalar))
-            for copy in copies:
-                copy()
-        last = len(CHUNKS) - 1
-        first = 0
-        for c, (t0, t1) in enumerate(CHUNKS):
-            if c == 2:
-                late = keep.tile([P, 2, T - t0], F32, name="late", tag="sums3_2", align_bytes=256)
-                y2, first = pick(2, t0, T, late[:]), t0
-            y3 = pick(3, t0, t1)
-            ring = (0, 1, 2) if c % 2 == 0 else (3, 5, 7)
-            edge = by_vector if c == last else by_scalar
-            ys = (y2[:, :, t0 - first : t1 - first], y3)
-            if c == last:
-                turn(2, c, ys[:1], banks[6][:, : t1 - t0], by_scalar)()
-                turn(3, c, ys[1:], banks[ring[0]][:, : t1 - t0], by_vector)()
+        head, middle, rest = GROUPS
+        for g, experts in enumerate((head, middle)):
+            for q in range(2):
+                first(q, experts, banks[4 * g + 2 * q])
+                second(q, experts, banks[4 * g + 2 * q + 1], parked=True)
+        for q in range(2):
+            first(q, rest, banks[2 * q])
+            second(q, rest, banks[2 * q + 1])
+            pick(q, GATED, TILES, gated=False)
+            pick(q, 0, GATED, gated=True)
+        early = ((2, middle), (2, rest), (2, head), (3, head))
+        for u, (q, experts) in enumerate(early):
+            first(q, experts, banks[2 + u])
+        for u, (q, experts) in enumerate(early):
+            second(q, experts, banks[(6 + u) % 8])
+        pick(2, 0, GATED, gated=True)
+        pick(2, GATED, TILES, gated=False)
+        for e in range(middle[0], E, 2):
+            first(3, (e, e + 2), banks[e - 2])
+            second(3, (e, e + 2), banks[e - 1])
+        pick(3, GATED, TILES, gated=False)
+        for j in range(GATED):
+            pick(3, j, j + 1, gated=True)
+        own = [banks[b] for b in (4, 5, 6, 0, 2)]
+        other = {3: banks[1], 4: banks[3]}
+        order = (0, 3, 1, 4, 2)
+        for j in (3, 4, 0, 1, 2):
+            if j < GATED:
+                turn_gated(0, 3, j, own[j][:, : 3 * P], by_scalar)()
             else:
-                turn(2, c, ys, banks[ring[0]][:, : 2 * (t1 - t0)], by_scalar)()
-            grouped = turn_back(c, banks[ring[1]], by_vector if c == last - 1 else by_scalar)
-            project(t0, t1, grouped, banks[ring[2]], edge)
+                turn_plain(0, 3, j, own[j][:, : 3 * P], other[j][:, : 3 * P])()
+        for j in order:
+            if j < GATED:
+                turn_gated(3, 4, j, own[j][:, 3 * P :], by_vector if j == 2 else by_scalar)()
+            else:
+                turn_plain(3, 4, j, own[j][:, 3 * P :], other[j][:, 3 * P :])()
+        for j in order:
+            finish(j, j + 1, own[j][:, 2 * P :], own[j], by_scalar, by_vector if j in (1, 2) else by_scalar)

@@ -112,6 +112,7 @@ def tile_moe_sdn_glu_relu_kernel(
             nc.scalar.copy(gate_t[:, r, :], bank[:, : GATED * P])
         for m in range(2):
             load_scales(m, 1, 0, E)
+        for m in range(2):
             load_words(m, *GROUPS[0], 2, 4)
         for e in range(GROUPS[1][0], E, 2):
             for m in range(2):
@@ -167,12 +168,6 @@ def tile_moe_sdn_glu_relu_kernel(
             sums = bank[:, : (experts[1] - experts[0]) * C]
             product(1, q, experts, sums)
             multiply(q, experts, sums, parked)
-
-        def both(q, experts, bank, parked=False):
-            for m in range(2):
-                product(m, q, experts, bank[:, 2 * C * m : 2 * C * (m + 1)])
-            activate(q, experts, bank[:, : 2 * C])
-            multiply(q, experts, bank[:, 2 * C :], parked)
 
         picked = {}
 

@@ -95,12 +95,13 @@ def tile_moe_sdn_glu_relu_kernel(
         load_words(0, *GROUPS[0], 0, 2)
         for m in range(2):
             load_scales(m, 0, 0, E)
+        for r, pos in enumerate((pos1, pos2)):
+            nc.sync.dma_start(pos_t[r][:], pos)
+        nc.sync.dma_start(w2w[:].bitcast(I32), w2_words[0].bitcast(I32))
         load_words(1, *GROUPS[0], 0, 2)
         for e in range(GROUPS[1][0], E, 2):
             for m in range(2):
                 load_words(m, e, e + 2, 0, 3)
-        for r, pos in enumerate((pos1, pos2)):
-            nc.sync.dma_start(pos_t[r][:], pos)
 
         nc.tensor.transpose(banks[0][:, :P], gate_rows[:], ident[:])
         nc.scalar.copy(gate_cols[:], banks[0][:, : 2 * TILES])
@@ -112,15 +113,14 @@ def tile_moe_sdn_glu_relu_kernel(
             nc.scalar.copy(gate_t[:, r, :], bank[:, : GATED * P])
         for m in range(2):
             load_scales(m, 1, 0, E)
+        w2_rows = w2_scales[0].rearrange("(b r) n -> r b n", r=4)
+        for r in range(4):
+            nc.sync.dma_start(w2s[r:P:32, :].bitcast(I32), w2_rows[r].bitcast(I32))
         for m in range(2):
             load_words(m, *GROUPS[0], 2, 4)
         for e in range(GROUPS[1][0], E, 2):
             for m in range(2):
                 load_words(m, e, e + 2, 3, 4)
-        nc.sync.dma_start(w2w[:].bitcast(I32), w2_words[0].bitcast(I32))
-        w2_rows = w2_scales[0].rearrange("(b r) n -> r b n", r=4)
-        for r in range(4):
-            nc.sync.dma_start(w2s[r:P:32, :].bitcast(I32), w2_rows[r].bitcast(I32))
 
         def gather_tokens(c0, c1):
             lst = offs_t[:, c0 // 16 : c1 // 16]

from contextlib import ExitStack

import concourse.mybir as mybir
from concourse.masks import make_identity

K, T, E, C, H, N = 1024, 640, 10, 128, 512, 256
FLOPS = 2 * 2 * K * H * E * C + 2 * H * N * T

F32 = mybir.dt.float32
BF16 = mybir.dt.bfloat16
I32 = mybir.dt.int32
U32 = mybir.dt.uint32
U16 = mybir.dt.uint16
U8 = mybir.dt.uint8
FP8X4 = mybir.dt.float8_e4m3fn_x4
FP4X4 = mybir.dt.float4_e2m1fn_x4
MULT = mybir.AluOpType.mult
ADD = mybir.AluOpType.add
RELU = mybir.ActivationFunctionType.Relu
COPY = mybir.ActivationFunctionType.Copy

P = 128
BANK = 512
S = E * C
PASSES = K // 512
HQ = H // P
TILES = T // P
GROUPS = ((0, 4), (4, 8), (8, 10))
GATED = 3
SPARE = 64


def tile_moe_sdn_glu_relu_kernel(
    tc, x_words, x_scales, w1_words, w1_scales, w3_words, w3_scales, w2_words, w2_scales, gate, offs, pos1, pos2, out
):
    nc = tc.nc
    with ExitStack() as ctx:
        keep = ctx.enter_context(tc.tile_pool(name="keep", bufs=1))
        psum = ctx.enter_context(tc.psum_pool(name="psum", bufs=1))
        banks = [psum.tile([P, BANK], F32, name=f"bank{b}") for b in range(8)]

        offs_t = keep.tile([P, S // 16], U16, name="offs_t")
        pos_t = [keep.tile([P, T // 16], U16, name=f"pos_t{r}") for r in range(2)]
        xw = keep.tile([P, PASSES * T + SPARE], I32, name="xw", align_bytes=256)
        xs = keep.tile([P, PASSES * T + SPARE], U8, name="xs", align_bytes=256)
        w2w = keep.tile([P, 2 * N], U8, name="w2w", align_bytes=256)
        w2s = keep.tile([P, N], U8, name="w2s", align_bytes=256)
        gate_t = keep.tile([P, 2, GATED * P], F32, name="gate_t")
        gate_cols = keep.tile([P, 2 * TILES], F32, name="gate_cols")
        ident = keep.tile([P, P], F32, name="ident")
        gx = [keep.tile([P, S], U32, name=f"gx{s}", align_bytes=256) for s in range(PASSES)]
        gs = [keep.tile([P, S], U8, name=f"gs{s}", align_bytes=256) for s in range(PASSES)]
        h = [keep.tile([P, S], F32, name=f"h{q}") for q in range(HQ)]
        ct = [keep.tile([P, H], BF16, name=f"ct{j}", align_bytes=256) for j in range(TILES)]
        planes = [
            [keep.tile([P, E * PASSES, 2 * P], U8, name=f"plane{half}_{m}", align_bytes=256) for m in range(2)]
            for half in range(2)
        ]
        words = {}

        nc.gpsimd.memset(xs[:].bitcast(I32), 0)
        gate_rows = keep.tile([P, P], F32, name="gate_rows")
        nc.gpsimd.memset(gate_rows[:], 0.0)
        make_identity(nc, ident[:])
        for pair in planes:
            for plane in pair:
                nc.vector.memset(plane[:].bitcast(I32), 0)
        nc.vector.memset(xw[:, PASSES * T :], 0)
        nc.vector.memset(w2s[:].bitcast(I32), 0)

        def load_words(m, e0, e1, q0, q1):
            rows = (w1_words, w3_words)[m][e0:e1].rearrange("e s p b -> p (e s) b")[:, :, 2 * P * q0 : 2 * P * q1]
            tile = keep.tile([P, (e1 - e0) * PASSES, 2 * P * (q1 - q0)], U8, name=f"words{m}_{e0}_{q0}", align_bytes=256)
            nc.sync.dma_start(tile[:].bitcast(I32), rows.bitcast(I32))
            for e in range(e0, e1):
                for q in range(q0, q1):
                    words[m, e, q] = tile[:, (e - e0) * PASSES : (e - e0 + 1) * PASSES, 2 * P * (q - q0) : 2 * P * (q - q0 + 1)]

        def load_scales(m, half, e0, e1):
            rows = (w1_scales, w3_scales)[m].rearrange("e s (b r) i -> r b (e s) i", r=4)
            for r in range(4):
                part = rows[r][:, e0 * PASSES : e1 * PASSES, 2 * P * half : 2 * P * (half + 1)]
                nc.sync.dma_start(planes[half][m][r:P:32, e0 * PASSES : e1 * PASSES, :].bitcast(I32), part.bitcast(I32))

        nc.sync.dma_start(
            xw[:, : PASSES * T].rearrange("p (s t) -> p s t", s=PASSES),
            x_words.rearrange("s p t d -> p s (t d)").bitcast(I32),
        )
        nc.sync.dma_start(offs_t[:], offs)
        xs_rows = x_scales.rearrange("s (b r) t -> r b s t", r=4)
        for r in range(4):
            rows = xs[r:P:32, : PASSES * T].rearrange("b (s t) -> b s t", s=PASSES)
            nc.scalar.dma_start(rows.bitcast(I32), xs_rows[r].bitcast(I32))
        nc.sync.dma_start(gate_rows[: 2 * TILES, :], gate[:, 0, :].rearrange("r (j t) -> r j t", t=P))
        load_words(0, *GROUPS[0], 0, 2)
        for m in range(2):
            load_scales(m, 0, 0, E)
        for r, pos in enumerate((pos1, pos2)):
            nc.sync.dma_start(pos_t[r][:], pos)
        nc.sync.dma_start(w2w[:].bitcast(I32), w2_words[0].bitcast(I32))
        load_words(1, *GROUPS[0], 0, 2)
        for e in range(GROUPS[1][0], E, 2):
            for m in range(2):
                load_words(m, e, e + 2, 0, 3)

        nc.tensor.transpose(banks[0][:, :P], gate_rows[:], ident[:])
        nc.scalar.copy(gate_cols[:], banks[0][:, : 2 * TILES])
        for r in range(2):
            bank = banks[4 + r]
            for j in range(GATED):
                column = gate_cols[:, r * TILES + j : r * TILES + j + 1]
                nc.tensor.transpose(bank[:, j * P : (j + 1) * P], column.to_broadcast([P, P]), ident[:])
            nc.scalar.copy(gate_t[:, r, :], bank[:, : GATED * P])
        for m in range(2):
            load_scales(m, 1, 0, E)
        w2_rows = w2_scales[0].rearrange("(b r) n -> r b n", r=4)
        for r in range(4):
            nc.sync.dma_start(w2s[r:P:32, :].bitcast(I32), w2_rows[r].bitcast(I32))
        for m in range(2):
            load_words(m, *GROUPS[0], 2, 4)
        for e in range(GROUPS[1][0], E, 2):
            for m in range(2):
                load_words(m, e, e + 2, 3, 4)

        def gather_tokens(c0, c1):
            lst = offs_t[:, c0 // 16 : c1 // 16]
            for s in range(PASSES):
                nc.vector.tensor_copy(gx[s][:, c0:c1], xw[:, s * T : (s + 1) * T + SPARE].bitcast(U32).indirect(lst))
            for s in range(PASSES):
                nc.vector.tensor_copy(gs[s][:, c0:c1], xs[:, s * T : (s + 1) * T + SPARE].indirect(lst))

        def product(m, q, experts, into):
            e0, e1 = experts
            for e in range(e0, e1):
                slots = slice(e * C, (e + 1) * C)
                for s in range(PASSES):
                    nc.tensor.matmul_mx(
                        out=into[:, (e - e0) * C : (e - e0 + 1) * C],
                        lhsT=words[m, e, q][:, s, :].bitcast(FP4X4),
                        lhsT_scale=planes[q // 2][m][:, e * PASSES + s, P * (q % 2) : P * (q % 2 + 1)],
                        rhs=gx[s][:, slots].bitcast(FP8X4),
                        rhs_scale=gs[s][:, slots],
                        start=(s == 0),
                        stop=(s == PASSES - 1),
                    )

        active = {}

        def activate(q, experts, sums):
            e0, e1 = experts
            active[q, e0] = keep.tile([P, (e1 - e0) * C], F32, name=f"active{q}_{e0}", align_bytes=256)
            nc.scalar.activation(active[q, e0][:], sums, RELU)

        def multiply(q, experts, sums, parked):
            e0, e1 = experts
            if parked:
                kept = keep.tile([P, (e1 - e0) * C], F32, name=f"parked{q}_{e0}", align_bytes=256)
                nc.scalar.copy(kept[:], sums)
                sums = kept[:]
            nc.vector.tensor_tensor(h[q][:, e0 * C : e1 * C], sums, active[q, e0][:], MULT)

        def first(q, experts, bank):
            sums = bank[:, : (experts[1] - experts[0]) * C]
            product(0, q, experts, sums)
            activate(q, experts, sums)

        def second(q, experts, bank, parked=False):
            sums = bank[:, : (experts[1] - experts[0]) * C]
            product(1, q, experts, sums)
            multiply(q, experts, sums, parked)

        picked = {}

        def pick(q, j0, j1, gated):
            t0, t1 = j0 * P, j1 * P
            y = keep.tile([P, 2, t1 - t0], F32, name=f"y{q}_{j0}", align_bytes=256)
            for r in range(2):
                found = h[q][:].indirect(pos_t[r][:, t0 // 16 : t1 // 16])
                if gated:
                    nc.vector.tensor_tensor(y[:, r, :], found, gate_t[:, r, t0:t1], MULT)
                else:
                    nc.scalar.activation(y[:, r, :], found, COPY)
            for j in range(j0, j1):
                picked[q, j] = y[:, :, (j - j0) * P : (j - j0 + 1) * P]

        def turn_gated(q0, q1, j, into, copy):
            for q in range(q0, q1):
                for r in range(2):
                    nc.tensor.matmul(
                        into[:, (q - q0) * P : (q - q0 + 1) * P],
                        lhsT=picked[q, j][:, r, :],
                        rhs=ident[:],
                        start=(r == 0),
                        stop=(r == 1),
                        is_transpose=True,
                    )
            return lambda: copy(
                ct[j][:].rearrange("t (u p e) -> t u p e", u=2, e=2)[:, :, 32 * q0 : 32 * q1, :],
                into.rearrange("t (p u e) -> t u p e", u=2, e=2),
            )

        def turn_plain(q0, q1, j, into_first, into_second):
            width = (q1 - q0) * P
            for q in range(q0, q1):
                for r, into in enumerate((into_first, into_second)):
                    nc.tensor.transpose(into[:, (q - q0) * P : (q - q0 + 1) * P], picked[q, j][:, r, :], ident[:])

            def combine():
                first = keep.tile([P, width], F32, name=f"first{q0}_{j}", align_bytes=256)
                nc.scalar.activation(first[:], into_first, COPY, scale=gate_cols[:, j : j + 1])
                nc.vector.scalar_tensor_tensor(
                    ct[j][:, q0 * P : q1 * P], into_second, gate_cols[:, TILES + j : TILES + j + 1], first[:], MULT, ADD
                )

            return combine

        out_v = out.rearrange("(a p) t -> p a t", p=P)

        def finish(j0, j1, back, bank, copy_back, copy_out):
            n = (j1 - j0) * P
            grouped = keep.tile([P, n, 4], BF16, name=f"grouped{j0}", align_bytes=256)
            for j in range(j0, j1):
                pairs = ct[j][:].bitcast(F32)
                for u in range(2):
                    b = 2 * (j - j0) + u
                    half = pairs[:, u * P : (u + 1) * P] if j < GATED else pairs[:, u : 2 * P : 2]
                    nc.tensor.transpose(back[:, b * P : (b + 1) * P], half, ident[:])
            copy_back(
                grouped[:].bitcast(F32).rearrange("p (j t) u -> p j t u", t=P),
                back[:, : 2 * n].rearrange("p (j u t) -> p j t u", u=2, t=P),
            )
            codes = keep.tile([P, n], U32, name=f"codes{j0}", align_bytes=256)
            cs = keep.tile([P, n], U8, name=f"cs{j0}", align_bytes=256)
            nc.vector.quantize_mx(out=codes[:].bitcast(FP8X4), scales=cs[:], in_=grouped[:].rearrange("p t j -> p (t j)"))
            for a in range(2):
                nc.tensor.matmul_mx(
                    out=bank[:, a * n : (a + 1) * n],
                    lhsT=w2w[:, 2 * P * a : 2 * P * (a + 1)].bitcast(FP4X4),
                    lhsT_scale=w2s[:, P * a : P * (a + 1)],
                    rhs=codes[:].bitcast(FP8X4),
                    rhs_scale=cs[:],
                    start=True,
                    stop=True,
                )
            res = keep.tile([P, 2, n], F32, name=f"res{j0}", align_bytes=256)
            copy_out(res[:], bank[:, : 2 * n].rearrange("p (a t) -> p a t", a=2))
            nc.sync.dma_start(out_v[:, :, j0 * P : j1 * P], res[:])

        by_scalar, by_vector = nc.scalar.copy, nc.vector.tensor_copy
        for e0, e1 in GROUPS:
            gather_tokens(e0 * C, e1 * C)
        head, middle, rest = GROUPS
        for g, experts in enumerate((head, middle)):
            for q in range(2):
                first(q, experts, banks[4 * g + 2 * q])
                second(q, experts, banks[4 * g + 2 * q + 1], parked=True)
        for q in range(2):
            first(q, rest, banks[2 * q])
            second(q, rest, banks[2 * q + 1])
            pick(q, GATED, TILES, gated=False)
            pick(q, 0, GATED, gated=True)
        early = ((2, middle), (2, rest), (2, head), (3, head))
        for u, (q, experts) in enumerate(early):
            first(q, experts, banks[2 + u])
        for u, (q, experts) in enumerate(early):
            second(q, experts, banks[(6 + u) % 8])
        pick(2, 0, GATED, gated=True)
        pick(2, GATED, TILES, gated=False)
        for e in range(middle[0], E, 2):
            first(3, (e, e + 2), banks[e - 2])
            second(3, (e, e + 2), banks[e - 1])
        pick(3, GATED, TILES, gated=False)
        for j in range(GATED):
            pick(3, j, j + 1, gated=True)
        own = [banks[b] for b in (4, 5, 6, 0, 2)]
        other = {3: banks[1], 4: banks[3]}
        order = (0, 3, 1, 4, 2)
        for j in (3, 4, 0, 1, 2):
            if j < GATED:
                turn_gated(0, 3, j, own[j][:, : 3 * P], by_scalar)()
            else:
                turn_plain(0, 3, j, own[j][:, : 3 * P], other[j][:, : 3 * P])()
        for j in order:
            if j < GATED:
                turn_gated(3, 4, j, own[j][:, 3 * P :], by_vector if j == 2 else by_scalar)()
            else:
                turn_plain(3, 4, j, own[j][:, 3 * P :], other[j][:, 3 * P :])()
        for j in order:
            finish(j, j + 1, own[j][:, 2 * P :], own[j], by_scalar, by_vector if j in (1, 2) else by_scalar)
